import numpy as np
import ml_dtypes


def mxq(x, axis, fmt="e4m3"):
    dtype, down = {"e4m3": (ml_dtypes.float8_e4m3fn, 7), "e5m2": (ml_dtypes.float8_e5m2, 14)}[fmt]
    v = np.moveaxis(np.asarray(x, np.float32).astype(ml_dtypes.bfloat16).astype(np.float64), axis, -1)
    blocks = v.reshape(v.shape[:-1] + (-1, 32))
    amax = np.abs(blocks).max(-1, keepdims=True)
    byte = np.maximum(np.where(amax > 0, np.frexp(amax)[1] - 1 + 127, 0) - down, 1)
    scale = np.exp2(byte - 127.0)
    codes = (blocks / scale).astype(np.float32).astype(dtype).astype(np.float64)
    return np.moveaxis((codes * scale).reshape(v.shape), -1, axis)


WIDE = False


def mx_kscale(k):
    if not WIDE:
        return np.ones(k)
    levels = np.array([10, -10, 5, -5, 0])
    if k % 512:
        return np.exp2(np.random.permutation(np.resize(levels, k // 32))).repeat(32)
    a = np.empty((k // 512, 16))
    for p in range(k // 512):
        a[p, :8] = np.random.permutation(np.resize(levels, 8))
        for g in range(8):
            far = levels[np.abs(levels - a[p, g]) >= 10]
            a[p, g + 8] = far[np.random.randint(len(far))]
    return np.exp2(a.ravel()).repeat(32)


def f64(x):
    return np.asarray(x).astype(np.float64)


def striped(idx):
    return np.tile(idx.reshape(-1, 16).T, (8, 1)).astype(np.uint16)


def unstriped(offs):
    return offs[:16].T.reshape(-1).astype(np.int64)


def pack_weight(w):
    k, n = w.shape
    w = f64(np.asarray(w, np.float32).astype(ml_dtypes.bfloat16)).reshape(k // 32, 32, n)
    amax = np.abs(w).max(1)
    byte = np.clip(np.where(amax > 0, np.frexp(amax)[1] - 1 + 127 - 7, 1), 1, 254)
    scaled = (w * np.exp2(127.0 - byte)[:, None, :]).reshape(k, n).astype(np.float32)
    words = np.ascontiguousarray(scaled.reshape(k // 512, 128, 4, n).transpose(0, 1, 3, 2)).astype(ml_dtypes.float8_e4m3fn).view(np.uint8)
    return words, np.ascontiguousarray(byte.astype(np.uint8).reshape(k // 512, 16, n))


def unpack_weight(words, scales):
    g, p, n, _ = words.shape
    vals = np.ascontiguousarray(words).view(ml_dtypes.float8_e4m3fn).astype(np.float64) * np.repeat(np.exp2(scales.astype(np.float64) - 127.0), 8, axis=1)[..., None]
    return vals.transpose(0, 1, 3, 2).reshape(g * 512, n)


def gelu(v):
    return 0.5 * v * (1.0 + np.tanh(np.sqrt(2.0 / np.pi) * (v + 0.044715 * v**3)))


K, T, E, C, N = 512, 512, 8, 128, 128


def by_expert(wq, xq):
    return np.concatenate([wq[e].T @ xq[:, e * C:(e + 1) * C] for e in range(E)], axis=1)


def setup_inputs():
    n = np.random.standard_normal
    s = mx_kscale(K)[:, None]
    first = np.random.permutation(np.repeat(np.arange(E), T // E))
    second = (first + 1 + np.random.permutation(np.repeat(np.arange(E - 1), -(-T // (E - 1)))[:T])) % E
    while np.bincount(second, minlength=E).max() != T // E:
        load = np.bincount(second, minlength=E); hi, lo = int(load.argmax()), int(load.argmin())
        t = np.flatnonzero((second == hi) & (first != lo))[0]; second[t] = lo
    slot_token = np.empty(E * C, np.int64); pos = np.empty((2, T), np.int64); fill = np.zeros(E, np.int64)
    place = np.stack([np.random.permutation(C) for _ in range(E)])
    for r, deal in enumerate((first, second)):
        for t in np.random.permutation(T):
            e = deal[t]; j = e * C + place[e, fill[e]]; fill[e] += 1; slot_token[j] = t; pos[r, t] = j
    g = np.random.uniform(0.2, 0.8, T)
    packed = [pack_weight(m) for m in n((E, K, N)) / np.sqrt(K) / s[None]]
    return {
        "xT": (n((K, T)) * s).astype(np.float32),
        "w_words": np.stack([m[0] for m in packed]),
        "w_scales": np.stack([m[1] for m in packed]),
        "b": (0.3 * n((N, E))).astype(np.float32),
        "gate": np.stack([np.tile(g, (N, 1)), np.tile(1.0 - g, (N, 1))]).astype(np.float32),
        "offs": striped(slot_token),
        "pos1": striped(pos[0]),
        "pos2": striped(pos[1]),
    }


def reference(xT, w_words, w_scales, b, gate, offs, pos1, pos2):
    idx = unstriped(offs)
    xq = mxq(f64(xT)[:, idx], 0, "e4m3")
    w = np.stack([unpack_weight(w_words[e], w_scales[e]) for e in range(E)])
    y = by_expert(w, xq)
    y = gelu(y + np.repeat(f64(b), C, axis=1))
    return f64(gate[0]) * y[:, unstriped(pos1)] + f64(gate[1]) * y[:, unstriped(pos2)]

@@ -1,0 +1,123 @@
+from contextlib import ExitStack
+
+import concourse.mybir as mybir
+
+K, T, E, C, N = 512, 512, 8, 128, 128
+P = 128
+SLOTS = E * C
+FLOPS = 2 * K * SLOTS * N
+
+F32 = mybir.dt.float32
+BF16 = mybir.dt.bfloat16
+I32 = mybir.dt.int32
+U32 = mybir.dt.uint32
+U16 = mybir.dt.uint16
+U8 = mybir.dt.uint8
+FP8X4 = mybir.dt.float8_e4m3fn_x4
+GELU = mybir.ActivationFunctionType.Gelu_apprx_tanh
+MULT = mybir.AluOpType.mult
+
+R = 4
+CHUNKS = ((0, 256, 168, ((0, 256),)), (256, 384, 80, ((0, 128),)), (384, 512, 80, ((0, 128),)))
+CODE_COLS = 1408
+SCALE_COLS = 704
+BYTE_CUTS = ((0, 512), (512, 768), (768, 896), (896, 1024))
+
+
+def tile_routed_moe_kernel(tc, xT, w_words, w_scales, b, gate, offs, pos1, pos2, out):
+    nc = tc.nc
+    with ExitStack() as ctx:
+        keep = ctx.enter_context(tc.tile_pool(name="keep", bufs=1))
+        psum = ctx.enter_context(tc.psum_pool(name="psum", bufs=1))
+
+        warm = keep.tile([P, 1], F32, name="warm")
+        nc.vector.memset(warm[:], 0.0)
+        nc.scalar.activation(warm[:], warm[:], GELU)
+
+        x_rows = xT.rearrange("(p r) w -> p r w", r=R)
+        raws = []
+        for lo, hi, vec, quants in CHUNKS:
+            raw = keep.tile([P, R, hi - lo], F32, name=f"raw{lo}")
+            nc.sync.dma_start(raw[:], x_rows[:, :, lo:hi])
+            raws.append(raw)
+
+        offs_t = keep.tile([P, SLOTS // 16], U16, name="offs_t")
+        nc.sync.dma_start(offs_t[:], offs)
+
+        w_s = keep.tile([P, E * N], U8, name="w_s", align_bytes=64)
+        nc.vector.memset(w_s[:].bitcast(I32), 0)
+        for q in range(4):
+            nc.sync.dma_start(
+                w_s[32 * q : 32 * q + 4, :].bitcast(I32).rearrange("p (e n) -> p e n", e=E),
+                w_scales[:, 0, 4 * q : 4 * q + 4, :].rearrange("e q n -> q e n").bitcast(I32),
+            )
+        w_c = keep.tile([P, E * N], U32, name="w_c", align_bytes=64)
+        nc.sync.dma_start(
+            w_c[:].bitcast(I32).rearrange("p (e n) -> p e n", e=E),
+            w_words.rearrange("e a p n r -> p (e a) (n r)").bitcast(I32),
+        )
+        b_t = keep.tile([P, E], F32, name="b_t")
+        nc.sync.dma_start(b_t[:], b)
+        pos1_t = keep.tile([P, T // 16], U16, name="pos1_t")
+        nc.sync.dma_start(pos1_t[:], pos1)
+        pos2_t = keep.tile([P, T // 16], U16, name="pos2_t")
+        nc.sync.dma_start(pos2_t[:], pos2)
+        gates = keep.tile([P, 2, T], F32, name="gates")
+        nc.sync.dma_start(gates[:], gate.rearrange("s p t -> p s t"))
+
+        codes = keep.tile([P, CODE_COLS], U32, name="codes", align_bytes=64)
+        scales = keep.tile([P, SCALE_COLS], U8, name="scales", align_bytes=64)
+        nc.gpsimd.memset(scales[:], 0)
+        nc.vector.memset(codes[:, T:].bitcast(I32), 0)
+
+        for (lo, hi, vec, quants), raw in zip(CHUNKS, raws):
+            grouped = keep.tile([P, hi - lo, R], BF16, name=f"grouped{lo}", align_bytes=64)
+            for copy, u, v in ((nc.scalar.copy, vec, hi - lo), (nc.vector.tensor_copy, 0, vec)):
+                copy(
+                    grouped[:, u:v, :].rearrange("p (c i) r -> p c r i", i=4),
+                    raw[:, :, u:v].rearrange("p r (c i) -> p c r i", i=4),
+                )
+            for u, v in quants:
+                nc.vector.quantize_mx(
+                    out=codes[:, lo + u : lo + v].bitcast(FP8X4),
+                    scales=scales[:, lo + u : lo + v],
+                    in_=grouped[:, u:v, :].rearrange("p w r -> p (w r)"),
+                )
+
+        slot_codes = keep.tile([P, SLOTS], U32, name="slot_codes", align_bytes=64)
+        slot_scales = keep.tile([P, SLOTS], U8, name="slot_scales", align_bytes=64)
+        nc.vector.tensor_copy(slot_codes[:], codes[:].indirect(offs_t[:]))
+        for lo, hi in BYTE_CUTS:
+            nc.vector.tensor_copy(slot_scales[:, lo:hi], scales[:].indirect(offs_t[:, lo // 16 : hi // 16]))
+
+        y = keep.tile([P, SLOTS], F32, name="y")
+        for e in range(E):
+            cols = slice(e * C, (e + 1) * C)
+            acc = psum.tile([N, C], F32, name=f"acc{e}")
+            nc.tensor.matmul_mx(
+                out=acc[:],
+                lhsT=w_c[:, cols].bitcast(FP8X4),
+                lhsT_scale=w_s[:, cols],
+                rhs=slot_codes[:, cols].bitcast(FP8X4),
+                rhs_scale=slot_scales[:, cols],
+                start=True,
+                stop=True,
+            )
+            nc.scalar.activation(y[:, cols], acc[:], GELU, bias=b_t[:, e : e + 1])
+
+        first = keep.tile([P, T], F32, name="first")
+        second = keep.tile([P, T], F32, name="second")
+        total = keep.tile([P, T], F32, name="total")
+        half = T // 2
+        nc.vector.tensor_tensor(first[:], y[:].indirect(pos1_t[:]), gates[:, 0, :], MULT)
+        for lo in (0, half):
+            nc.vector.tensor_tensor(
+                second[:, lo : lo + half],
+                y[:].indirect(pos2_t[:, lo // 16 : (lo + half) // 16]),
+                gates[:, 1, lo : lo + half],
+                MULT,
+            )
+        for lo in (0, half):
+            cols = slice(lo, lo + half)
+            nc.vector.tensor_add(total[:, cols], first[:, cols], second[:, cols])
+            nc.sync.dma_start(out[:, cols], total[:, cols])

@@ -18,7 +18,10 @@ GELU = mybir.ActivationFunctionType.Gelu_apprx_tanh
 MULT = mybir.AluOpType.mult
 
 R = 4
-CHUNKS = ((0, 256, 168, ((0, 256),)), (256, 384, 80, ((0, 128),)), (384, 512, 80, ((0, 128),)))
+HALVES = ((0, 256), (256, 512))
+LOW_VEC = 320
+HIGH_VEC = 96
+QUANT = 128
 CODE_COLS = 1408
 SCALE_COLS = 704
 BYTE_CUTS = ((0, 512), (512, 768), (768, 896), (896, 1024))
@@ -35,11 +38,13 @@ def tile_routed_moe_kernel(tc, xT, w_words, w_scales, b, gate, offs, pos1, pos2,
         nc.scalar.activation(warm[:], warm[:], GELU)
 
         x_rows = xT.rearrange("(p r) w -> p r w", r=R)
-        raws = []
-        for lo, hi, vec, quants in CHUNKS:
-            raw = keep.tile([P, R, hi - lo], F32, name=f"raw{lo}")
-            nc.sync.dma_start(raw[:], x_rows[:, :, lo:hi])
-            raws.append(raw)
+        low = keep.tile([P, 2, T], F32, name="low")
+        nc.sync.dma_start(low[:], x_rows[:, 0:2, :])
+        highs = []
+        for lo, hi in HALVES:
+            high = keep.tile([P, 2, hi - lo], F32, name=f"high{lo}")
+            nc.sync.dma_start(high[:], x_rows[:, 2:4, lo:hi])
+            highs.append(high)
 
         offs_t = keep.tile([P, SLOTS // 16], U16, name="offs_t")
         nc.sync.dma_start(offs_t[:], offs)
@@ -70,18 +75,18 @@ def tile_routed_moe_kernel(tc, xT, w_words, w_scales, b, gate, offs, pos1, pos2,
         nc.gpsimd.memset(scales[:], 0)
         nc.vector.memset(codes[:, T:].bitcast(I32), 0)
 
-        for (lo, hi, vec, quants), raw in zip(CHUNKS, raws):
-            grouped = keep.tile([P, hi - lo, R], BF16, name=f"grouped{lo}", align_bytes=64)
-            for copy, u, v in ((nc.scalar.copy, vec, hi - lo), (nc.vector.tensor_copy, 0, vec)):
-                copy(
-                    grouped[:, u:v, :].rearrange("p (c i) r -> p c r i", i=4),
-                    raw[:, :, u:v].rearrange("p r (c i) -> p c r i", i=4),
-                )
-            for u, v in quants:
+        grouped = keep.tile([P, T, R], BF16, name="grouped", align_bytes=64)
+        for copy, u, v in ((nc.scalar.copy, LOW_VEC, T), (nc.vector.tensor_copy, 0, LOW_VEC)):
+            copy(grouped[:, u:v, 0:2], low[:, :, u:v].rearrange("p r w -> p w r"))
+        for (lo, hi), high in zip(HALVES, highs):
+            for copy, a, z in ((nc.scalar.copy, HIGH_VEC, QUANT), (nc.vector.tensor_copy, 0, HIGH_VEC)):
+                for u in range(0, hi - lo, QUANT):
+                    copy(grouped[:, lo + u + a : lo + u + z, 2:4], high[:, :, u + a : u + z].rearrange("p r w -> p w r"))
+            for u in range(lo, hi, QUANT):
                 nc.vector.quantize_mx(
-                    out=codes[:, lo + u : lo + v].bitcast(FP8X4),
-                    scales=scales[:, lo + u : lo + v],
-                    in_=grouped[:, u:v, :].rearrange("p w r -> p (w r)"),
+                    out=codes[:, u : u + QUANT].bitcast(FP8X4),
+                    scales=scales[:, u : u + QUANT],
+                    in_=grouped[:, u : u + QUANT, :].rearrange("p w r -> p (w r)"),
                 )
 
         slot_codes = keep.tile([P, SLOTS], U32, name="slot_codes", align_bytes=64)

@@ -18,13 +18,9 @@ GELU = mybir.ActivationFunctionType.Gelu_apprx_tanh
 MULT = mybir.AluOpType.mult
 
 R = 4
-HALVES = ((0, 256), (256, 512))
-LOW_VEC = 320
-HIGH_VEC = 96
-QUANT = 128
-CODE_COLS = 1408
-SCALE_COLS = 704
-BYTE_CUTS = ((0, 512), (512, 768), (768, 896), (896, 1024))
+LOW_COLS = 1408
+LOW_VEC = 340
+PIECES = ((0, 256), (256, 512), (512, 640), (640, 768), (768, 896), (896, 1024))
 
 
 def tile_routed_moe_kernel(tc, xT, w_words, w_scales, b, gate, offs, pos1, pos2, out):
@@ -40,14 +36,10 @@ def tile_routed_moe_kernel(tc, xT, w_words, w_scales, b, gate, offs, pos1, pos2,
         x_rows = xT.rearrange("(p r) w -> p r w", r=R)
         low = keep.tile([P, 2, T], F32, name="low")
         nc.sync.dma_start(low[:], x_rows[:, 0:2, :])
-        highs = []
-        for lo, hi in HALVES:
-            high = keep.tile([P, 2, hi - lo], F32, name=f"high{lo}")
-            nc.sync.dma_start(high[:], x_rows[:, 2:4, lo:hi])
-            highs.append(high)
-
         offs_t = keep.tile([P, SLOTS // 16], U16, name="offs_t")
         nc.sync.dma_start(offs_t[:], offs)
+        high = keep.tile([P, 2, T], F32, name="high")
+        nc.sync.dma_start(high[:], x_rows[:, 2:4, :])
 
         w_s = keep.tile([P, E * N], U8, name="w_s", align_bytes=64)
         nc.vector.memset(w_s[:].bitcast(I32), 0)
@@ -70,45 +62,46 @@ def tile_routed_moe_kernel(tc, xT, w_words, w_scales, b, gate, offs, pos1, pos2,
         gates = keep.tile([P, 2, T], F32, name="gates")
         nc.sync.dma_start(gates[:], gate.rearrange("s p t -> p s t"))
 
-        codes = keep.tile([P, CODE_COLS], U32, name="codes", align_bytes=64)
-        scales = keep.tile([P, SCALE_COLS], U8, name="scales", align_bytes=64)
-        nc.gpsimd.memset(scales[:], 0)
-        nc.vector.memset(codes[:, T:].bitcast(I32), 0)
-
-        grouped = keep.tile([P, T, R], BF16, name="grouped", align_bytes=64)
+        low_pairs = keep.tile([P, LOW_COLS], I32, name="low_pairs")
+        high_pairs = keep.tile([P, T], I32, name="high_pairs")
+        nc.vector.memset(low_pairs[:, T:], 0)
         for copy, u, v in ((nc.scalar.copy, LOW_VEC, T), (nc.vector.tensor_copy, 0, LOW_VEC)):
-            copy(grouped[:, u:v, 0:2], low[:, :, u:v].rearrange("p r w -> p w r"))
-        for (lo, hi), high in zip(HALVES, highs):
-            for copy, a, z in ((nc.scalar.copy, HIGH_VEC, QUANT), (nc.vector.tensor_copy, 0, HIGH_VEC)):
-                for u in range(0, hi - lo, QUANT):
-                    copy(grouped[:, lo + u + a : lo + u + z, 2:4], high[:, :, u + a : u + z].rearrange("p r w -> p w r"))
-            for u in range(lo, hi, QUANT):
-                nc.vector.quantize_mx(
-                    out=codes[:, u : u + QUANT].bitcast(FP8X4),
-                    scales=scales[:, u : u + QUANT],
-                    in_=grouped[:, u : u + QUANT, :].rearrange("p w r -> p (w r)"),
-                )
+            copy(
+                low_pairs[:, u:v].bitcast(BF16).rearrange("p (w r) -> p w r", r=2),
+                low[:, :, u:v].rearrange("p r w -> p w r"),
+            )
+        nc.scalar.copy(
+            high_pairs[:].bitcast(BF16).rearrange("p (w r) -> p w r", r=2),
+            high[:].rearrange("p r w -> p w r"),
+        )
 
+        picked = keep.tile([P, 2, SLOTS], U32, name="picked")
+        grouped = keep.tile([P, SLOTS, 2], U32, name="grouped", align_bytes=64)
         slot_codes = keep.tile([P, SLOTS], U32, name="slot_codes", align_bytes=64)
         slot_scales = keep.tile([P, SLOTS], U8, name="slot_scales", align_bytes=64)
-        nc.vector.tensor_copy(slot_codes[:], codes[:].indirect(offs_t[:]))
-        for lo, hi in BYTE_CUTS:
-            nc.vector.tensor_copy(slot_scales[:, lo:hi], scales[:].indirect(offs_t[:, lo // 16 : hi // 16]))
-
         y = keep.tile([P, SLOTS], F32, name="y")
-        for e in range(E):
-            cols = slice(e * C, (e + 1) * C)
-            acc = psum.tile([N, C], F32, name=f"acc{e}")
-            nc.tensor.matmul_mx(
-                out=acc[:],
-                lhsT=w_c[:, cols].bitcast(FP8X4),
-                lhsT_scale=w_s[:, cols],
-                rhs=slot_codes[:, cols].bitcast(FP8X4),
-                rhs_scale=slot_scales[:, cols],
-                start=True,
-                stop=True,
+        nc.vector.tensor_copy(picked[:, 0, :], low_pairs[:].bitcast(U32).indirect(offs_t[:]))
+        for lo, hi in PIECES:
+            nc.vector.tensor_copy(picked[:, 1, lo:hi], high_pairs[:].bitcast(U32).indirect(offs_t[:, lo // 16 : hi // 16]))
+            nc.scalar.copy(grouped[:, lo:hi, :], picked[:, :, lo:hi].rearrange("p u s -> p s u"))
+            nc.vector.quantize_mx(
+                out=slot_codes[:, lo:hi].bitcast(FP8X4),
+                scales=slot_scales[:, lo:hi],
+                in_=grouped[:, lo:hi, :].rearrange("p s u -> p (s u)").bitcast(BF16),
             )
-            nc.scalar.activation(y[:, cols], acc[:], GELU, bias=b_t[:, e : e + 1])
+            for e in range(lo // C, hi // C):
+                cols = slice(e * C, (e + 1) * C)
+                acc = psum.tile([N, C], F32, name=f"acc{e}")
+                nc.tensor.matmul_mx(
+                    out=acc[:],
+                    lhsT=w_c[:, cols].bitcast(FP8X4),
+                    lhsT_scale=w_s[:, cols],
+                    rhs=slot_codes[:, cols].bitcast(FP8X4),
+                    rhs_scale=slot_scales[:, cols],
+                    start=True,
+                    stop=True,
+                )
+                nc.scalar.activation(y[:, cols], acc[:], GELU, bias=b_t[:, e : e + 1])
 
         first = keep.tile([P, T], F32, name="first")
         second = keep.tile([P, T], F32, name="second")

@@ -15,11 +15,14 @@ U16 = mybir.dt.uint16
 U8 = mybir.dt.uint8
 FP8X4 = mybir.dt.float8_e4m3fn_x4
 GELU = mybir.ActivationFunctionType.Gelu_apprx_tanh
+COPY = mybir.ActivationFunctionType.Copy
 MULT = mybir.AluOpType.mult
+ADD = mybir.AluOpType.add
 
 R = 4
-LOW_COLS = 1408
+LOW_COLS = 1024
 LOW_VEC = 340
+VEC_SLOTS = 768
 PIECES = ((0, 256), (256, 512), (512, 640), (640, 768), (768, 896), (896, 1024))
 
 
@@ -70,9 +73,15 @@ def tile_routed_moe_kernel(tc, xT, w_words, w_scales, b, gate, offs, pos1, pos2,
                 low_pairs[:, u:v].bitcast(BF16).rearrange("p (w r) -> p w r", r=2),
                 low[:, :, u:v].rearrange("p r w -> p w r"),
             )
-        nc.scalar.copy(
+        low_planes = keep.tile([P, 2, T], BF16, name="low_planes")
+        nc.scalar.copy(low_planes[:], low[:])
+        nc.gpsimd.tensor_scalar(
             high_pairs[:].bitcast(BF16).rearrange("p (w r) -> p w r", r=2),
             high[:].rearrange("p r w -> p w r"),
+            1.0,
+            0.0,
+            MULT,
+            ADD,
         )
 
         picked = keep.tile([P, 2, SLOTS], U32, name="picked")
@@ -80,10 +89,14 @@ def tile_routed_moe_kernel(tc, xT, w_words, w_scales, b, gate, offs, pos1, pos2,
         slot_codes = keep.tile([P, SLOTS], U32, name="slot_codes", align_bytes=64)
         slot_scales = keep.tile([P, SLOTS], U8, name="slot_scales", align_bytes=64)
         y = keep.tile([P, SLOTS], F32, name="y")
-        nc.vector.tensor_copy(picked[:, 0, :], low_pairs[:].bitcast(U32).indirect(offs_t[:]))
+        nc.vector.tensor_copy(picked[:, 0, :VEC_SLOTS], low_pairs[:].bitcast(U32).indirect(offs_t[:, : VEC_SLOTS // 16]))
+        halves = picked[:, 0, VEC_SLOTS:].bitcast(BF16).rearrange("p (s r) -> p s r", r=2)
+        for r in range(2):
+            nc.scalar.activation(halves[:, :, r], low_planes[:, r, :].indirect(offs_t[:, VEC_SLOTS // 16 :]), COPY)
         for lo, hi in PIECES:
             nc.vector.tensor_copy(picked[:, 1, lo:hi], high_pairs[:].bitcast(U32).indirect(offs_t[:, lo // 16 : hi // 16]))
             nc.scalar.copy(grouped[:, lo:hi, :], picked[:, :, lo:hi].rearrange("p u s -> p s u"))
+        for lo, hi in PIECES:
             nc.vector.quantize_mx(
                 out=slot_codes[:, lo:hi].bitcast(FP8X4),
                 scales=slot_scales[:, lo:hi],

@@ -20,10 +20,13 @@ MULT = mybir.AluOpType.mult
 ADD = mybir.AluOpType.add
 
 R = 4
-LOW_COLS = 1024
+LOW_COLS = 896
 LOW_VEC = 340
-VEC_SLOTS = 768
-PIECES = ((0, 256), (256, 512), (512, 640), (640, 768), (768, 896), (896, 1024))
+VEC_SLOTS = 640
+GATHERS = ((0, 128), (128, 512), (512, 704), (704, 864), (864, 1024))
+POOL_WEAVES = ((0, 128), (128, 256))
+SCALAR_WEAVES = ((256, 512), (512, 704), (704, 864), (864, 1024))
+PIECES = ((0, 256), (256, 512), (512, 768), (768, 896), (896, 1024))
 
 
 def tile_routed_moe_kernel(tc, xT, w_words, w_scales, b, gate, offs, pos1, pos2, out):
@@ -41,8 +44,11 @@ def tile_routed_moe_kernel(tc, xT, w_words, w_scales, b, gate, offs, pos1, pos2,
         nc.sync.dma_start(low[:], x_rows[:, 0:2, :])
         offs_t = keep.tile([P, SLOTS // 16], U16, name="offs_t")
         nc.sync.dma_start(offs_t[:], offs)
-        high = keep.tile([P, 2, T], F32, name="high")
-        nc.sync.dma_start(high[:], x_rows[:, 2:4, :])
+        highs = []
+        for lo in (0, T // 2):
+            high = keep.tile([P, 2, T // 2], F32, name=f"high{lo}")
+            nc.sync.dma_start(high[:], x_rows[:, 2:4, lo : lo + T // 2])
+            highs.append(high)
 
         w_s = keep.tile([P, E * N], U8, name="w_s", align_bytes=64)
         nc.vector.memset(w_s[:].bitcast(I32), 0)
@@ -75,14 +81,15 @@ def tile_routed_moe_kernel(tc, xT, w_words, w_scales, b, gate, offs, pos1, pos2,
             )
         low_planes = keep.tile([P, 2, T], BF16, name="low_planes")
         nc.scalar.copy(low_planes[:], low[:])
-        nc.gpsimd.tensor_scalar(
-            high_pairs[:].bitcast(BF16).rearrange("p (w r) -> p w r", r=2),
-            high[:].rearrange("p r w -> p w r"),
-            1.0,
-            0.0,
-            MULT,
-            ADD,
-        )
+        for lo, high in zip((0, T // 2), highs):
+            nc.gpsimd.tensor_scalar(
+                high_pairs[:, lo : lo + T // 2].bitcast(BF16).rearrange("p (w r) -> p w r", r=2),
+                high[:].rearrange("p r w -> p w r"),
+                1.0,
+                0.0,
+                MULT,
+                ADD,
+            )
 
         picked = keep.tile([P, 2, SLOTS], U32, name="picked")
         grouped = keep.tile([P, SLOTS, 2], U32, name="grouped", align_bytes=64)
@@ -93,8 +100,18 @@ def tile_routed_moe_kernel(tc, xT, w_words, w_scales, b, gate, offs, pos1, pos2,
         halves = picked[:, 0, VEC_SLOTS:].bitcast(BF16).rearrange("p (s r) -> p s r", r=2)
         for r in range(2):
             nc.scalar.activation(halves[:, :, r], low_planes[:, r, :].indirect(offs_t[:, VEC_SLOTS // 16 :]), COPY)
-        for lo, hi in PIECES:
+        for lo, hi in GATHERS:
             nc.vector.tensor_copy(picked[:, 1, lo:hi], high_pairs[:].bitcast(U32).indirect(offs_t[:, lo // 16 : hi // 16]))
+        for lo, hi in POOL_WEAVES:
+            nc.gpsimd.tensor_scalar(
+                grouped[:, lo:hi, :].bitcast(BF16).rearrange("p s (u r) -> p s u r", r=2),
+                picked[:, :, lo:hi].bitcast(BF16).rearrange("p u (s r) -> p s u r", r=2),
+                1.0,
+                0.0,
+                MULT,
+                ADD,
+            )
+        for lo, hi in SCALAR_WEAVES:
             nc.scalar.copy(grouped[:, lo:hi, :], picked[:, :, lo:hi].rearrange("p u s -> p s u"))
         for lo, hi in PIECES:
             nc.vector.quantize_mx(

@@ -20,9 +20,10 @@ MULT = mybir.AluOpType.mult
 ADD = mybir.AluOpType.add
 
 R = 4
-LOW_COLS = 896
-LOW_VEC = 340
+HALF = T // 2
 VEC_SLOTS = 640
+LOW_COLS = 896
+SHARE = 128
 GATHERS = ((0, 128), (128, 512), (512, 704), (704, 864), (864, 1024))
 POOL_WEAVES = ((0, 128), (128, 256))
 SCALAR_WEAVES = ((256, 512), (512, 704), (704, 864), (864, 1024))
@@ -41,14 +42,14 @@ def tile_routed_moe_kernel(tc, xT, w_words, w_scales, b, gate, offs, pos1, pos2,
 
         x_rows = xT.rearrange("(p r) w -> p r w", r=R)
         low = keep.tile([P, 2, T], F32, name="low")
-        nc.sync.dma_start(low[:], x_rows[:, 0:2, :])
+        for r in range(2):
+            nc.sync.dma_start(low[:, r, :], x_rows[:, r, :])
         offs_t = keep.tile([P, SLOTS // 16], U16, name="offs_t")
         nc.sync.dma_start(offs_t[:], offs)
-        highs = []
-        for lo in (0, T // 2):
-            high = keep.tile([P, 2, T // 2], F32, name=f"high{lo}")
-            nc.sync.dma_start(high[:], x_rows[:, 2:4, lo : lo + T // 2])
-            highs.append(high)
+        early = keep.tile([P, 2, HALF], F32, name="early")
+        nc.sync.dma_start(early[:], x_rows[:, 2:4, HALF:])
+        late = keep.tile([P, 2, HALF], F32, name="late")
+        nc.sync.dma_start(late[:], x_rows[:, 2:4, :HALF])
 
         w_s = keep.tile([P, E * N], U8, name="w_s", align_bytes=64)
         nc.vector.memset(w_s[:].bitcast(I32), 0)
@@ -72,24 +73,22 @@ def tile_routed_moe_kernel(tc, xT, w_words, w_scales, b, gate, offs, pos1, pos2,
         nc.sync.dma_start(gates[:], gate.rearrange("s p t -> p s t"))
 
         low_pairs = keep.tile([P, LOW_COLS], I32, name="low_pairs")
-        high_pairs = keep.tile([P, T], I32, name="high_pairs")
         nc.vector.memset(low_pairs[:, T:], 0)
-        for copy, u, v in ((nc.scalar.copy, LOW_VEC, T), (nc.vector.tensor_copy, 0, LOW_VEC)):
-            copy(
-                low_pairs[:, u:v].bitcast(BF16).rearrange("p (w r) -> p w r", r=2),
-                low[:, :, u:v].rearrange("p r w -> p w r"),
-            )
-        low_planes = keep.tile([P, 2, T], BF16, name="low_planes")
-        nc.scalar.copy(low_planes[:], low[:])
-        for lo, high in zip((0, T // 2), highs):
-            nc.gpsimd.tensor_scalar(
-                high_pairs[:, lo : lo + T // 2].bitcast(BF16).rearrange("p (w r) -> p w r", r=2),
-                high[:].rearrange("p r w -> p w r"),
-                1.0,
-                0.0,
-                MULT,
-                ADD,
-            )
+        plane0 = keep.tile([P, T], BF16, name="plane0")
+        mixed = keep.tile([P, HALF + T], I32, name="mixed")
+        plane1 = mixed[:, : HALF + SHARE].bitcast(BF16)
+        high_pairs = mixed[:, HALF:]
+
+        def halves(words):
+            return words.bitcast(BF16).rearrange("p (w r) -> p w r", r=2)
+
+        for r, plane in enumerate((plane0[:], plane1[:, :T])):
+            nc.vector.tensor_copy(halves(low_pairs[:, :T])[:, :, r], low[:, r, :])
+            nc.scalar.copy(plane, low[:, r, :])
+        nc.gpsimd.tensor_scalar(halves(high_pairs[:, HALF:]), early[:].rearrange("p r w -> p w r"), 1.0, 0.0, MULT, ADD)
+        nc.gpsimd.tensor_scalar(
+            halves(high_pairs[:, SHARE:HALF]), late[:, :, SHARE:].rearrange("p r w -> p w r"), 1.0, 0.0, MULT, ADD
+        )
 
         picked = keep.tile([P, 2, SLOTS], U32, name="picked")
         grouped = keep.tile([P, SLOTS, 2], U32, name="grouped", align_bytes=64)
@@ -97,11 +96,13 @@ def tile_routed_moe_kernel(tc, xT, w_words, w_scales, b, gate, offs, pos1, pos2,
         slot_scales = keep.tile([P, SLOTS], U8, name="slot_scales", align_bytes=64)
         y = keep.tile([P, SLOTS], F32, name="y")
         nc.vector.tensor_copy(picked[:, 0, :VEC_SLOTS], low_pairs[:].bitcast(U32).indirect(offs_t[:, : VEC_SLOTS // 16]))
-        halves = picked[:, 0, VEC_SLOTS:].bitcast(BF16).rearrange("p (s r) -> p s r", r=2)
-        for r in range(2):
-            nc.scalar.activation(halves[:, :, r], low_planes[:, r, :].indirect(offs_t[:, VEC_SLOTS // 16 :]), COPY)
+        rest = halves(picked[:, 0, VEC_SLOTS:])
+        nc.scalar.activation(rest[:, :, 0], plane0[:].indirect(offs_t[:, VEC_SLOTS // 16 :]), COPY)
+        nc.scalar.copy(halves(high_pairs[:, :SHARE]), late[:, :, :SHARE].rearrange("p r w -> p w r"))
+        nc.scalar.activation(rest[:, :, 1], plane1.indirect(offs_t[:, VEC_SLOTS // 16 :]), COPY)
+
         for lo, hi in GATHERS:
-            nc.vector.tensor_copy(picked[:, 1, lo:hi], high_pairs[:].bitcast(U32).indirect(offs_t[:, lo // 16 : hi // 16]))
+            nc.vector.tensor_copy(picked[:, 1, lo:hi], high_pairs.bitcast(U32).indirect(offs_t[:, lo // 16 : hi // 16]))
         for lo, hi in POOL_WEAVES:
             nc.gpsimd.tensor_scalar(
                 grouped[:, lo:hi, :].bitcast(BF16).rearrange("p s (u r) -> p s u r", r=2),

@@ -21,8 +21,9 @@ ADD = mybir.AluOpType.add
 
 R = 4
 HALF = T // 2
-VEC_SLOTS = 640
-LOW_COLS = 896
+VEC_SLOTS = 512
+LOW_COLS = 704
+PLANE_COLS = 704
 SHARE = 128
 GATHERS = ((0, 128), (128, 512), (512, 704), (704, 864), (864, 1024))
 POOL_WEAVES = ((0, 128), (128, 256))
@@ -42,10 +43,10 @@ def tile_routed_moe_kernel(tc, xT, w_words, w_scales, b, gate, offs, pos1, pos2,
 
         x_rows = xT.rearrange("(p r) w -> p r w", r=R)
         low = keep.tile([P, 2, T], F32, name="low")
-        for r in range(2):
-            nc.sync.dma_start(low[:, r, :], x_rows[:, r, :])
         offs_t = keep.tile([P, SLOTS // 16], U16, name="offs_t")
+        nc.sync.dma_start(low[:, 0, :], x_rows[:, 0, :])
         nc.sync.dma_start(offs_t[:], offs)
+        nc.sync.dma_start(low[:, 1, :], x_rows[:, 1, :])
         early = keep.tile([P, 2, HALF], F32, name="early")
         nc.sync.dma_start(early[:], x_rows[:, 2:4, HALF:])
         late = keep.tile([P, 2, HALF], F32, name="late")
@@ -74,7 +75,8 @@ def tile_routed_moe_kernel(tc, xT, w_words, w_scales, b, gate, offs, pos1, pos2,
 
         low_pairs = keep.tile([P, LOW_COLS], I32, name="low_pairs")
         nc.vector.memset(low_pairs[:, T:], 0)
-        plane0 = keep.tile([P, T], BF16, name="plane0")
+        plane0 = keep.tile([P, PLANE_COLS], BF16, name="plane0")
+        nc.vector.memset(plane0[:, T:].bitcast(I32), 0)
         mixed = keep.tile([P, HALF + T], I32, name="mixed")
         plane1 = mixed[:, : HALF + SHARE].bitcast(BF16)
         high_pairs = mixed[:, HALF:]
@@ -82,9 +84,10 @@ def tile_routed_moe_kernel(tc, xT, w_words, w_scales, b, gate, offs, pos1, pos2,
         def halves(words):
             return words.bitcast(BF16).rearrange("p (w r) -> p w r", r=2)
 
-        for r, plane in enumerate((plane0[:], plane1[:, :T])):
+        nc.vector.tensor_copy(plane0[:, :T], low[:, 0, :])
+        for r in range(2):
             nc.vector.tensor_copy(halves(low_pairs[:, :T])[:, :, r], low[:, r, :])
-            nc.scalar.copy(plane, low[:, r, :])
+        nc.vector.tensor_copy(plane1[:, :T], low[:, 1, :])
         nc.gpsimd.tensor_scalar(halves(high_pairs[:, HALF:]), early[:].rearrange("p r w -> p w r"), 1.0, 0.0, MULT, ADD)
         nc.gpsimd.tensor_scalar(
             halves(high_pairs[:, SHARE:HALF]), late[:, :, SHARE:].rearrange("p r w -> p w r"), 1.0, 0.0, MULT, ADD

@@ -21,13 +21,13 @@ ADD = mybir.AluOpType.add
 
 R = 4
 HALF = T // 2
-VEC_SLOTS = 512
-LOW_COLS = 704
-PLANE_COLS = 704
+VEC_SLOTS = 544
+LOW_COLS = 736
+PLANE_COLS = 640
 SHARE = 128
-GATHERS = ((0, 128), (128, 512), (512, 704), (704, 864), (864, 1024))
-POOL_WEAVES = ((0, 128), (128, 256))
-SCALAR_WEAVES = ((256, 512), (512, 704), (704, 864), (864, 1024))
+GATHERS = ((0, 224), (224, 512), (512, 800), (800, 1024))
+POOL_WEAVES = GATHERS[:1]
+SCALAR_WEAVES = GATHERS[1:]
 PIECES = ((0, 256), (256, 512), (512, 768), (768, 896), (896, 1024))
 
 
@@ -107,14 +107,7 @@ def tile_routed_moe_kernel(tc, xT, w_words, w_scales, b, gate, offs, pos1, pos2,
         for lo, hi in GATHERS:
             nc.vector.tensor_copy(picked[:, 1, lo:hi], high_pairs.bitcast(U32).indirect(offs_t[:, lo // 16 : hi // 16]))
         for lo, hi in POOL_WEAVES:
-            nc.gpsimd.tensor_scalar(
-                grouped[:, lo:hi, :].bitcast(BF16).rearrange("p s (u r) -> p s u r", r=2),
-                picked[:, :, lo:hi].bitcast(BF16).rearrange("p u (s r) -> p s u r", r=2),
-                1.0,
-                0.0,
-                MULT,
-                ADD,
-            )
+            nc.gpsimd.tensor_copy(grouped[:, lo:hi, :], picked[:, :, lo:hi].rearrange("p u s -> p s u"))
         for lo, hi in SCALAR_WEAVES:
             nc.scalar.copy(grouped[:, lo:hi, :], picked[:, :, lo:hi].rearrange("p u s -> p s u"))
         for lo, hi in PIECES:

@@ -21,14 +21,15 @@ ADD = mybir.AluOpType.add
 
 R = 4
 HALF = T // 2
-VEC_SLOTS = 544
-LOW_COLS = 736
-PLANE_COLS = 640
-SHARE = 128
-GATHERS = ((0, 224), (224, 512), (512, 800), (800, 1024))
-POOL_WEAVES = GATHERS[:1]
-SCALAR_WEAVES = GATHERS[1:]
-PIECES = ((0, 256), (256, 512), (512, 768), (768, 896), (896, 1024))
+VEC_EARLY = 288
+VEC_SLOTS = 416
+PLANE_COLS = 832
+PAD = 32
+SHARE = 129
+GATHERS = ((0, 256), (256, 448), (448, 640), (640, 832), (832, 1024))
+POOL_WEAVES = ((0, 256),)
+SCALAR_WEAVES = ((256, 448), (448, 640), (640, 832), (832, 896), (896, 1024))
+PIECES = ((0, 128), (128, 256), (256, 384), (384, 512), (512, 640), (640, 768), (768, 896), (896, 1024))
 
 
 def tile_routed_moe_kernel(tc, xT, w_words, w_scales, b, gate, offs, pos1, pos2, out):
@@ -49,8 +50,10 @@ def tile_routed_moe_kernel(tc, xT, w_words, w_scales, b, gate, offs, pos1, pos2,
         nc.sync.dma_start(low[:, 1, :], x_rows[:, 1, :])
         early = keep.tile([P, 2, HALF], F32, name="early")
         nc.sync.dma_start(early[:], x_rows[:, 2:4, HALF:])
-        late = keep.tile([P, 2, HALF], F32, name="late")
-        nc.sync.dma_start(late[:], x_rows[:, 2:4, :HALF])
+        low_late = keep.tile([P, 2 * T], I32, name="low_late")
+        low_pairs = low_late[:, :T]
+        late = low_late[:, T:].bitcast(F32).rearrange("p (r w) -> p r w", r=2)
+        nc.sync.dma_start(late, x_rows[:, 2:4, :HALF])
 
         w_s = keep.tile([P, E * N], U8, name="w_s", align_bytes=64)
         nc.vector.memset(w_s[:].bitcast(I32), 0)
@@ -73,32 +76,33 @@ def tile_routed_moe_kernel(tc, xT, w_words, w_scales, b, gate, offs, pos1, pos2,
         gates = keep.tile([P, 2, T], F32, name="gates")
         nc.sync.dma_start(gates[:], gate.rearrange("s p t -> p s t"))
 
-        low_pairs = keep.tile([P, LOW_COLS], I32, name="low_pairs")
-        nc.vector.memset(low_pairs[:, T:], 0)
         plane0 = keep.tile([P, PLANE_COLS], BF16, name="plane0")
         nc.vector.memset(plane0[:, T:].bitcast(I32), 0)
-        mixed = keep.tile([P, HALF + T], I32, name="mixed")
-        plane1 = mixed[:, : HALF + SHARE].bitcast(BF16)
-        high_pairs = mixed[:, HALF:]
+        mixed = keep.tile([P, HALF + PAD + T], I32, name="mixed")
+        nc.vector.memset(mixed[:, HALF : HALF + PAD], 0)
+        plane1 = mixed[:, : HALF + PAD + SHARE - 1].bitcast(BF16)
+        high_pairs = mixed[:, HALF + PAD :]
 
         def halves(words):
             return words.bitcast(BF16).rearrange("p (w r) -> p w r", r=2)
 
         nc.vector.tensor_copy(plane0[:, :T], low[:, 0, :])
         for r in range(2):
-            nc.vector.tensor_copy(halves(low_pairs[:, :T])[:, :, r], low[:, r, :])
+            nc.vector.tensor_copy(halves(low_pairs)[:, :, r], low[:, r, :])
         nc.vector.tensor_copy(plane1[:, :T], low[:, 1, :])
         nc.gpsimd.tensor_scalar(halves(high_pairs[:, HALF:]), early[:].rearrange("p r w -> p w r"), 1.0, 0.0, MULT, ADD)
-        nc.gpsimd.tensor_scalar(
-            halves(high_pairs[:, SHARE:HALF]), late[:, :, SHARE:].rearrange("p r w -> p w r"), 1.0, 0.0, MULT, ADD
-        )
 
         picked = keep.tile([P, 2, SLOTS], U32, name="picked")
         grouped = keep.tile([P, SLOTS, 2], U32, name="grouped", align_bytes=64)
         slot_codes = keep.tile([P, SLOTS], U32, name="slot_codes", align_bytes=64)
         slot_scales = keep.tile([P, SLOTS], U8, name="slot_scales", align_bytes=64)
         y = keep.tile([P, SLOTS], F32, name="y")
-        nc.vector.tensor_copy(picked[:, 0, :VEC_SLOTS], low_pairs[:].bitcast(U32).indirect(offs_t[:, : VEC_SLOTS // 16]))
+        nc.vector.tensor_copy(picked[:, 0, :VEC_EARLY], low_pairs.bitcast(U32).indirect(offs_t[:, : VEC_EARLY // 16]))
+        nc.vector.tensor_copy(halves(high_pairs[:, SHARE:HALF]), late[:, :, SHARE:].rearrange("p r w -> p w r"))
+        nc.vector.tensor_copy(
+            picked[:, 0, VEC_EARLY:VEC_SLOTS],
+            low_late[:, : T + 16].bitcast(U32).indirect(offs_t[:, VEC_EARLY // 16 : VEC_SLOTS // 16]),
+        )
         rest = halves(picked[:, 0, VEC_SLOTS:])
         nc.scalar.activation(rest[:, :, 0], plane0[:].indirect(offs_t[:, VEC_SLOTS // 16 :]), COPY)
         nc.scalar.copy(halves(high_pairs[:, :SHARE]), late[:, :, :SHARE].rearrange("p r w -> p w r"))

@@ -21,6 +21,8 @@ ADD = mybir.AluOpType.add
 
 R = 4
 HALF = T // 2
+LAST = 256
+POOL_FROM = 256
 VEC_EARLY = 288
 VEC_SLOTS = 416
 PLANE_COLS = 832
@@ -48,12 +50,13 @@ def tile_routed_moe_kernel(tc, xT, w_words, w_scales, b, gate, offs, pos1, pos2,
         nc.sync.dma_start(low[:, 0, :], x_rows[:, 0, :])
         nc.sync.dma_start(offs_t[:], offs)
         nc.sync.dma_start(low[:, 1, :], x_rows[:, 1, :])
-        early = keep.tile([P, 2, HALF], F32, name="early")
-        nc.sync.dma_start(early[:], x_rows[:, 2:4, HALF:])
-        low_late = keep.tile([P, 2 * T], I32, name="low_late")
+        x_runs = xT.rearrange("(p r) w -> p (r w)", r=R)
+        low_late = keep.tile([P, 3 * T], I32, name="low_late")
         low_pairs = low_late[:, :T]
-        late = low_late[:, T:].bitcast(F32).rearrange("p (r w) -> p r w", r=2)
-        nc.sync.dma_start(late, x_rows[:, 2:4, :HALF])
+        high_run = low_late[:, T:].bitcast(F32)
+        nc.sync.dma_start(high_run[:, LAST:], x_runs[:, 2 * T + LAST :])
+        nc.sync.dma_start(high_run[:, :LAST], x_runs[:, 2 * T : 2 * T + LAST])
+        high_rows = high_run.rearrange("p (r w) -> p w r", r=2)
 
         w_s = keep.tile([P, E * N], U8, name="w_s", align_bytes=64)
         nc.vector.memset(w_s[:].bitcast(I32), 0)
@@ -90,7 +93,7 @@ def tile_routed_moe_kernel(tc, xT, w_words, w_scales, b, gate, offs, pos1, pos2,
         for r in range(2):
             nc.vector.tensor_copy(halves(low_pairs)[:, :, r], low[:, r, :])
         nc.vector.tensor_copy(plane1[:, :T], low[:, 1, :])
-        nc.gpsimd.tensor_scalar(halves(high_pairs[:, HALF:]), early[:].rearrange("p r w -> p w r"), 1.0, 0.0, MULT, ADD)
+        nc.gpsimd.tensor_scalar(halves(high_pairs[:, POOL_FROM:]), high_rows[:, POOL_FROM:, :], 1.0, 0.0, MULT, ADD)
 
         picked = keep.tile([P, 2, SLOTS], U32, name="picked")
         grouped = keep.tile([P, SLOTS, 2], U32, name="grouped", align_bytes=64)
@@ -98,14 +101,14 @@ def tile_routed_moe_kernel(tc, xT, w_words, w_scales, b, gate, offs, pos1, pos2,
         slot_scales = keep.tile([P, SLOTS], U8, name="slot_scales", align_bytes=64)
         y = keep.tile([P, SLOTS], F32, name="y")
         nc.vector.tensor_copy(picked[:, 0, :VEC_EARLY], low_pairs.bitcast(U32).indirect(offs_t[:, : VEC_EARLY // 16]))
-        nc.vector.tensor_copy(halves(high_pairs[:, SHARE:HALF]), late[:, :, SHARE:].rearrange("p r w -> p w r"))
+        nc.vector.tensor_copy(halves(high_pairs[:, SHARE:POOL_FROM]), high_rows[:, SHARE:POOL_FROM, :])
         nc.vector.tensor_copy(
             picked[:, 0, VEC_EARLY:VEC_SLOTS],
             low_late[:, : T + 16].bitcast(U32).indirect(offs_t[:, VEC_EARLY // 16 : VEC_SLOTS // 16]),
         )
         rest = halves(picked[:, 0, VEC_SLOTS:])
         nc.scalar.activation(rest[:, :, 0], plane0[:].indirect(offs_t[:, VEC_SLOTS // 16 :]), COPY)
-        nc.scalar.copy(halves(high_pairs[:, :SHARE]), late[:, :, :SHARE].rearrange("p r w -> p w r"))
+        nc.scalar.copy(halves(high_pairs[:, :SHARE]), high_rows[:, :SHARE, :])
         nc.scalar.activation(rest[:, :, 1], plane1.indirect(offs_t[:, VEC_SLOTS // 16 :]), COPY)
 
         for lo, hi in GATHERS:

@@ -23,10 +23,10 @@ R = 4
 HALF = T // 2
 LAST = 256
 POOL_FROM = 256
-VEC_EARLY = 288
-VEC_SLOTS = 416
-PLANE_COLS = 832
-PAD = 32
+VEC_EARLY = 320
+VEC_SLOTS = 448
+PLANE_COLS = 768
+ROW0_COLS = 608
 SHARE = 129
 GATHERS = ((0, 256), (256, 448), (448, 640), (640, 832), (832, 1024))
 POOL_WEAVES = ((0, 256),)
@@ -45,15 +45,15 @@ def tile_routed_moe_kernel(tc, xT, w_words, w_scales, b, gate, offs, pos1, pos2,
         nc.scalar.activation(warm[:], warm[:], GELU)
 
         x_rows = xT.rearrange("(p r) w -> p r w", r=R)
-        low = keep.tile([P, 2, T], F32, name="low")
-        offs_t = keep.tile([P, SLOTS // 16], U16, name="offs_t")
-        nc.sync.dma_start(low[:, 0, :], x_rows[:, 0, :])
-        nc.sync.dma_start(offs_t[:], offs)
-        nc.sync.dma_start(low[:, 1, :], x_rows[:, 1, :])
         x_runs = xT.rearrange("(p r) w -> p (r w)", r=R)
-        low_late = keep.tile([P, 3 * T], I32, name="low_late")
-        low_pairs = low_late[:, :T]
-        high_run = low_late[:, T:].bitcast(F32)
+        row0 = keep.tile([P, ROW0_COLS], F32, name="row0")
+        nc.vector.memset(row0[:, T:], 0.0)
+        rest_rows = keep.tile([P, 3 * T], F32, name="rest_rows")
+        high_run = rest_rows[:, T:]
+        offs_t = keep.tile([P, SLOTS // 16], U16, name="offs_t")
+        nc.sync.dma_start(row0[:, :T], x_rows[:, 0, :])
+        nc.sync.dma_start(offs_t[:], offs)
+        nc.sync.dma_start(rest_rows[:, :T], x_rows[:, 1, :])
         nc.sync.dma_start(high_run[:, LAST:], x_runs[:, 2 * T + LAST :])
         nc.sync.dma_start(high_run[:, :LAST], x_runs[:, 2 * T : 2 * T + LAST])
         high_rows = high_run.rearrange("p (r w) -> p w r", r=2)
@@ -81,18 +81,15 @@ def tile_routed_moe_kernel(tc, xT, w_words, w_scales, b, gate, offs, pos1, pos2,
 
         plane0 = keep.tile([P, PLANE_COLS], BF16, name="plane0")
         nc.vector.memset(plane0[:, T:].bitcast(I32), 0)
-        mixed = keep.tile([P, HALF + PAD + T], I32, name="mixed")
-        nc.vector.memset(mixed[:, HALF : HALF + PAD], 0)
-        plane1 = mixed[:, : HALF + PAD + SHARE - 1].bitcast(BF16)
-        high_pairs = mixed[:, HALF + PAD :]
+        mixed = keep.tile([P, HALF + T], I32, name="mixed")
+        plane1 = mixed[:, : HALF + SHARE - 1].bitcast(BF16)
+        high_pairs = mixed[:, HALF:]
 
         def halves(words):
             return words.bitcast(BF16).rearrange("p (w r) -> p w r", r=2)
 
-        nc.vector.tensor_copy(plane0[:, :T], low[:, 0, :])
-        for r in range(2):
-            nc.vector.tensor_copy(halves(low_pairs)[:, :, r], low[:, r, :])
-        nc.vector.tensor_copy(plane1[:, :T], low[:, 1, :])
+        nc.vector.tensor_copy(plane0[:, :T], row0[:, :T])
+        nc.gpsimd.tensor_scalar(plane1[:, :T], rest_rows[:, :T], 1.0, 0.0, MULT, ADD)
         nc.gpsimd.tensor_scalar(halves(high_pairs[:, POOL_FROM:]), high_rows[:, POOL_FROM:, :], 1.0, 0.0, MULT, ADD)
 
         picked = keep.tile([P, 2, SLOTS], U32, name="picked")
@@ -100,11 +97,12 @@ def tile_routed_moe_kernel(tc, xT, w_words, w_scales, b, gate, offs, pos1, pos2,
         slot_codes = keep.tile([P, SLOTS], U32, name="slot_codes", align_bytes=64)
         slot_scales = keep.tile([P, SLOTS], U8, name="slot_scales", align_bytes=64)
         y = keep.tile([P, SLOTS], F32, name="y")
-        nc.vector.tensor_copy(picked[:, 0, :VEC_EARLY], low_pairs.bitcast(U32).indirect(offs_t[:, : VEC_EARLY // 16]))
+        own = halves(picked[:, 0, :VEC_SLOTS])
+        nc.vector.tensor_copy(own[:, :, 0], row0[:].indirect(offs_t[:, : VEC_SLOTS // 16]))
+        nc.vector.tensor_copy(own[:, :VEC_EARLY, 1], rest_rows[:, :T].indirect(offs_t[:, : VEC_EARLY // 16]))
         nc.vector.tensor_copy(halves(high_pairs[:, SHARE:POOL_FROM]), high_rows[:, SHARE:POOL_FROM, :])
         nc.vector.tensor_copy(
-            picked[:, 0, VEC_EARLY:VEC_SLOTS],
-            low_late[:, : T + 16].bitcast(U32).indirect(offs_t[:, VEC_EARLY // 16 : VEC_SLOTS // 16]),
+            own[:, VEC_EARLY:, 1], rest_rows[:, : T + 16].indirect(offs_t[:, VEC_EARLY // 16 : VEC_SLOTS // 16])
         )
         rest = halves(picked[:, 0, VEC_SLOTS:])
         nc.scalar.activation(rest[:, :, 0], plane0[:].indirect(offs_t[:, VEC_SLOTS // 16 :]), COPY)

@@ -21,16 +21,12 @@ ADD = mybir.AluOpType.add
 
 R = 4
 HALF = T // 2
-LAST = 256
-POOL_FROM = 256
-VEC_EARLY = 320
-VEC_SLOTS = 448
-PLANE_COLS = 768
-ROW0_COLS = 608
-SHARE = 129
-GATHERS = ((0, 256), (256, 448), (448, 640), (640, 832), (832, 1024))
-POOL_WEAVES = ((0, 256),)
-SCALAR_WEAVES = ((256, 448), (448, 640), (640, 832), (832, 896), (896, 1024))
+VEC_SLOTS = 320
+VEC_EARLY = 192
+SCALAR_GATHERS = ((320, 672), (672, 1024))
+GATHERS = ((0, 288), (288, 512), (512, 704), (704, 896), (896, 1024))
+POOL_WEAVES = ((0, 288),)
+SCALAR_WEAVES = ((288, 512), (512, 704), (704, 896), (896, 1024))
 PIECES = ((0, 128), (128, 256), (256, 384), (384, 512), (512, 640), (640, 768), (768, 896), (896, 1024))
 
 
@@ -45,18 +41,15 @@ def tile_routed_moe_kernel(tc, xT, w_words, w_scales, b, gate, offs, pos1, pos2,
         nc.scalar.activation(warm[:], warm[:], GELU)
 
         x_rows = xT.rearrange("(p r) w -> p r w", r=R)
-        x_runs = xT.rearrange("(p r) w -> p (r w)", r=R)
-        row0 = keep.tile([P, ROW0_COLS], F32, name="row0")
-        nc.vector.memset(row0[:, T:], 0.0)
-        rest_rows = keep.tile([P, 3 * T], F32, name="rest_rows")
-        high_run = rest_rows[:, T:]
+        raw = keep.tile([P, R, T], F32, name="raw")
         offs_t = keep.tile([P, SLOTS // 16], U16, name="offs_t")
-        nc.sync.dma_start(row0[:, :T], x_rows[:, 0, :])
+        nc.sync.dma_start(raw[:, 0, :], x_rows[:, 0, :])
         nc.sync.dma_start(offs_t[:], offs)
-        nc.sync.dma_start(rest_rows[:, :T], x_rows[:, 1, :])
-        nc.sync.dma_start(high_run[:, LAST:], x_runs[:, 2 * T + LAST :])
-        nc.sync.dma_start(high_run[:, :LAST], x_runs[:, 2 * T : 2 * T + LAST])
-        high_rows = high_run.rearrange("p (r w) -> p w r", r=2)
+        nc.sync.dma_start(raw[:, 1, :], x_rows[:, 1, :])
+        x_runs = xT.rearrange("(p r) w -> p (r w)", r=R)
+        rows = raw[:].rearrange("p r w -> p (r w)")
+        nc.sync.dma_start(rows[:, 2 * T + HALF :], x_runs[:, 2 * T + HALF :])
+        nc.sync.dma_start(rows[:, 2 * T : 2 * T + HALF], x_runs[:, 2 * T : 2 * T + HALF])
 
         w_s = keep.tile([P, E * N], U8, name="w_s", align_bytes=64)
         nc.vector.memset(w_s[:].bitcast(I32), 0)
@@ -79,35 +72,38 @@ def tile_routed_moe_kernel(tc, xT, w_words, w_scales, b, gate, offs, pos1, pos2,
         gates = keep.tile([P, 2, T], F32, name="gates")
         nc.sync.dma_start(gates[:], gate.rearrange("s p t -> p s t"))
 
-        plane0 = keep.tile([P, PLANE_COLS], BF16, name="plane0")
-        nc.vector.memset(plane0[:, T:].bitcast(I32), 0)
-        mixed = keep.tile([P, HALF + T], I32, name="mixed")
-        plane1 = mixed[:, : HALF + SHARE - 1].bitcast(BF16)
-        high_pairs = mixed[:, HALF:]
-
-        def halves(words):
-            return words.bitcast(BF16).rearrange("p (w r) -> p w r", r=2)
-
-        nc.vector.tensor_copy(plane0[:, :T], row0[:, :T])
-        nc.gpsimd.tensor_scalar(plane1[:, :T], rest_rows[:, :T], 1.0, 0.0, MULT, ADD)
-        nc.gpsimd.tensor_scalar(halves(high_pairs[:, POOL_FROM:]), high_rows[:, POOL_FROM:, :], 1.0, 0.0, MULT, ADD)
-
+        plane0 = keep.tile([P, T], BF16, name="plane0")
+        plane1 = keep.tile([P, T], BF16, name="plane1")
+        high_t = keep.tile([P, T], I32, name="high_t")
+        high_pairs = high_t[:]
         picked = keep.tile([P, 2, SLOTS], U32, name="picked")
         grouped = keep.tile([P, SLOTS, 2], U32, name="grouped", align_bytes=64)
         slot_codes = keep.tile([P, SLOTS], U32, name="slot_codes", align_bytes=64)
         slot_scales = keep.tile([P, SLOTS], U8, name="slot_scales", align_bytes=64)
         y = keep.tile([P, SLOTS], F32, name="y")
-        own = halves(picked[:, 0, :VEC_SLOTS])
-        nc.vector.tensor_copy(own[:, :, 0], row0[:].indirect(offs_t[:, : VEC_SLOTS // 16]))
-        nc.vector.tensor_copy(own[:, :VEC_EARLY, 1], rest_rows[:, :T].indirect(offs_t[:, : VEC_EARLY // 16]))
-        nc.vector.tensor_copy(halves(high_pairs[:, SHARE:POOL_FROM]), high_rows[:, SHARE:POOL_FROM, :])
+
+        def halves(words):
+            return words.bitcast(BF16).rearrange("p (w r) -> p w r", r=2)
+
+        def entries(lo, hi):
+            return offs_t[:, lo // 16 : hi // 16]
+
+        def cast_high(lo, hi):
+            return halves(high_pairs[:, lo:hi]), raw[:, 2:4, lo:hi].rearrange("p r w -> p w r")
+
+        low = halves(picked[:, 0, :])
+        nc.vector.tensor_copy(plane0[:], raw[:, 0, :])
+        nc.gpsimd.tensor_scalar(plane1[:], raw[:, 1, :], 1.0, 0.0, MULT, ADD)
+        nc.vector.tensor_copy(low[:, :VEC_SLOTS, 0], raw[:, 0, :].indirect(entries(0, VEC_SLOTS)))
+        nc.vector.tensor_copy(low[:, :VEC_EARLY, 1], raw[:, 1, :].indirect(entries(0, VEC_EARLY)))
+        nc.vector.tensor_copy(*cast_high(HALF, T))
+        nc.vector.tensor_copy(*cast_high(0, HALF))
         nc.vector.tensor_copy(
-            own[:, VEC_EARLY:, 1], rest_rows[:, : T + 16].indirect(offs_t[:, VEC_EARLY // 16 : VEC_SLOTS // 16])
+            low[:, VEC_EARLY:VEC_SLOTS, 1], rows[:, T : 2 * T + 16].indirect(entries(VEC_EARLY, VEC_SLOTS))
         )
-        rest = halves(picked[:, 0, VEC_SLOTS:])
-        nc.scalar.activation(rest[:, :, 0], plane0[:].indirect(offs_t[:, VEC_SLOTS // 16 :]), COPY)
-        nc.scalar.copy(halves(high_pairs[:, :SHARE]), high_rows[:, :SHARE, :])
-        nc.scalar.activation(rest[:, :, 1], plane1.indirect(offs_t[:, VEC_SLOTS // 16 :]), COPY)
+        for r, plane in enumerate((plane0, plane1)):
+            for lo, hi in SCALAR_GATHERS:
+                nc.scalar.activation(low[:, lo:hi, r], plane[:].indirect(entries(lo, hi)), COPY)
 
         for lo, hi in GATHERS:
             nc.vector.tensor_copy(picked[:, 1, lo:hi], high_pairs.bitcast(U32).indirect(offs_t[:, lo // 16 : hi // 16]))

@@ -22,7 +22,7 @@ ADD = mybir.AluOpType.add
 R = 4
 HALF = T // 2
 VEC_SLOTS = 320
-VEC_EARLY = 192
+VEC_EARLY = 224
 SCALAR_GATHERS = ((320, 672), (672, 1024))
 GATHERS = ((0, 288), (288, 512), (512, 704), (704, 896), (896, 1024))
 POOL_WEAVES = ((0, 288),)

@@ -21,12 +21,12 @@ ADD = mybir.AluOpType.add
 
 R = 4
 HALF = T // 2
-VEC_SLOTS = 320
-VEC_EARLY = 224
-SCALAR_GATHERS = ((320, 672), (672, 1024))
-GATHERS = ((0, 288), (288, 512), (512, 704), (704, 896), (896, 1024))
-POOL_WEAVES = ((0, 288),)
-SCALAR_WEAVES = ((288, 512), (512, 704), (704, 896), (896, 1024))
+VEC_SLOTS = 288
+DIRECT_HIGH = ((0, 352),)
+SCALAR_GATHERS = ((288, 672), (672, 1024))
+GATHERS = ((352, 576), (576, 800), (800, 1024))
+POOL_WEAVES = ((0, 352),)
+SCALAR_WEAVES = ((352, 576), (576, 800), (800, 1024))
 PIECES = ((0, 128), (128, 256), (256, 384), (384, 512), (512, 640), (640, 768), (768, 896), (896, 1024))
 
 
@@ -92,21 +92,23 @@ def tile_routed_moe_kernel(tc, xT, w_words, w_scales, b, gate, offs, pos1, pos2,
             return halves(high_pairs[:, lo:hi]), raw[:, 2:4, lo:hi].rearrange("p r w -> p w r")
 
         low = halves(picked[:, 0, :])
-        nc.vector.tensor_copy(plane0[:], raw[:, 0, :])
+        high = halves(picked[:, 1, :])
+        nc.vector.tensor_copy(plane0[:, :HALF], raw[:, 0, :HALF])
+        nc.scalar.copy(plane0[:, HALF:], raw[:, 0, HALF:])
         nc.gpsimd.tensor_scalar(plane1[:], raw[:, 1, :], 1.0, 0.0, MULT, ADD)
-        nc.vector.tensor_copy(low[:, :VEC_SLOTS, 0], raw[:, 0, :].indirect(entries(0, VEC_SLOTS)))
-        nc.vector.tensor_copy(low[:, :VEC_EARLY, 1], raw[:, 1, :].indirect(entries(0, VEC_EARLY)))
-        nc.vector.tensor_copy(*cast_high(HALF, T))
-        nc.vector.tensor_copy(*cast_high(0, HALF))
-        nc.vector.tensor_copy(
-            low[:, VEC_EARLY:VEC_SLOTS, 1], rows[:, T : 2 * T + 16].indirect(entries(VEC_EARLY, VEC_SLOTS))
-        )
+        nc.gpsimd.tensor_scalar(*cast_high(HALF, T), 1.0, 0.0, MULT, ADD)
+        nc.gpsimd.tensor_scalar(*cast_high(0, HALF), 1.0, 0.0, MULT, ADD)
+        for r in (0, 1):
+            nc.vector.tensor_copy(low[:, :VEC_SLOTS, r], raw[:, r, :].indirect(entries(0, VEC_SLOTS)))
+        for r in (3, 2):
+            for lo, hi in DIRECT_HIGH:
+                nc.vector.tensor_copy(high[:, lo:hi, r - 2], raw[:, r, :].indirect(entries(lo, hi)))
         for r, plane in enumerate((plane0, plane1)):
             for lo, hi in SCALAR_GATHERS:
                 nc.scalar.activation(low[:, lo:hi, r], plane[:].indirect(entries(lo, hi)), COPY)
 
         for lo, hi in GATHERS:
-            nc.vector.tensor_copy(picked[:, 1, lo:hi], high_pairs.bitcast(U32).indirect(offs_t[:, lo // 16 : hi // 16]))
+            nc.vector.tensor_copy(picked[:, 1, lo:hi], high_pairs.bitcast(U32).indirect(entries(lo, hi)))
         for lo, hi in POOL_WEAVES:
             nc.gpsimd.tensor_copy(grouped[:, lo:hi, :], picked[:, :, lo:hi].rearrange("p u s -> p s u"))
         for lo, hi in SCALAR_WEAVES:

@@ -21,9 +21,10 @@ ADD = mybir.AluOpType.add
 
 R = 4
 HALF = T // 2
-VEC_SLOTS = 288
+LAST = 384
+VEC_SLOTS = 256
 DIRECT_HIGH = ((0, 352),)
-SCALAR_GATHERS = ((288, 672), (672, 1024))
+SCALAR_GATHERS = ((256, 640), (640, 1024))
 GATHERS = ((352, 576), (576, 800), (800, 1024))
 POOL_WEAVES = ((0, 352),)
 SCALAR_WEAVES = ((352, 576), (576, 800), (800, 1024))
@@ -48,8 +49,8 @@ def tile_routed_moe_kernel(tc, xT, w_words, w_scales, b, gate, offs, pos1, pos2,
         nc.sync.dma_start(raw[:, 1, :], x_rows[:, 1, :])
         x_runs = xT.rearrange("(p r) w -> p (r w)", r=R)
         rows = raw[:].rearrange("p r w -> p (r w)")
-        nc.sync.dma_start(rows[:, 2 * T + HALF :], x_runs[:, 2 * T + HALF :])
-        nc.sync.dma_start(rows[:, 2 * T : 2 * T + HALF], x_runs[:, 2 * T : 2 * T + HALF])
+        nc.sync.dma_start(rows[:, 2 * T + LAST :], x_runs[:, 2 * T + LAST :])
+        nc.sync.dma_start(rows[:, 2 * T : 2 * T + LAST], x_runs[:, 2 * T : 2 * T + LAST])
 
         w_s = keep.tile([P, E * N], U8, name="w_s", align_bytes=64)
         nc.vector.memset(w_s[:].bitcast(I32), 0)
@@ -96,8 +97,8 @@ def tile_routed_moe_kernel(tc, xT, w_words, w_scales, b, gate, offs, pos1, pos2,
         nc.vector.tensor_copy(plane0[:, :HALF], raw[:, 0, :HALF])
         nc.scalar.copy(plane0[:, HALF:], raw[:, 0, HALF:])
         nc.gpsimd.tensor_scalar(plane1[:], raw[:, 1, :], 1.0, 0.0, MULT, ADD)
-        nc.gpsimd.tensor_scalar(*cast_high(HALF, T), 1.0, 0.0, MULT, ADD)
-        nc.gpsimd.tensor_scalar(*cast_high(0, HALF), 1.0, 0.0, MULT, ADD)
+        nc.gpsimd.tensor_scalar(*cast_high(LAST, T), 1.0, 0.0, MULT, ADD)
+        nc.gpsimd.tensor_scalar(*cast_high(0, LAST), 1.0, 0.0, MULT, ADD)
         for r in (0, 1):
             nc.vector.tensor_copy(low[:, :VEC_SLOTS, r], raw[:, r, :].indirect(entries(0, VEC_SLOTS)))
         for r in (3, 2):

@@ -22,12 +22,13 @@ ADD = mybir.AluOpType.add
 R = 4
 HALF = T // 2
 LAST = 384
+VEC_CAST = 320
 VEC_SLOTS = 256
 DIRECT_HIGH = ((0, 352),)
 SCALAR_GATHERS = ((256, 640), (640, 1024))
 GATHERS = ((352, 576), (576, 800), (800, 1024))
-POOL_WEAVES = ((0, 352),)
-SCALAR_WEAVES = ((352, 576), (576, 800), (800, 1024))
+POOL_WEAVES = ((0, 352), (352, 416))
+SCALAR_WEAVES = ((416, 576), (576, 800), (800, 1024))
 PIECES = ((0, 128), (128, 256), (256, 384), (384, 512), (512, 640), (640, 768), (768, 896), (896, 1024))
 
 
@@ -94,8 +95,8 @@ def tile_routed_moe_kernel(tc, xT, w_words, w_scales, b, gate, offs, pos1, pos2,
 
         low = halves(picked[:, 0, :])
         high = halves(picked[:, 1, :])
-        nc.vector.tensor_copy(plane0[:, :HALF], raw[:, 0, :HALF])
-        nc.scalar.copy(plane0[:, HALF:], raw[:, 0, HALF:])
+        nc.vector.tensor_copy(plane0[:, :VEC_CAST], raw[:, 0, :VEC_CAST])
+        nc.scalar.copy(plane0[:, VEC_CAST:], raw[:, 0, VEC_CAST:])
         nc.gpsimd.tensor_scalar(plane1[:], raw[:, 1, :], 1.0, 0.0, MULT, ADD)
         nc.gpsimd.tensor_scalar(*cast_high(LAST, T), 1.0, 0.0, MULT, ADD)
         nc.gpsimd.tensor_scalar(*cast_high(0, LAST), 1.0, 0.0, MULT, ADD)

@@ -26,9 +26,9 @@ VEC_CAST = 320
 VEC_SLOTS = 256
 DIRECT_HIGH = ((0, 352),)
 SCALAR_GATHERS = ((256, 640), (640, 1024))
-GATHERS = ((352, 576), (576, 800), (800, 1024))
+GATHERS = ((352, 608), (608, 832), (832, 1024))
 POOL_WEAVES = ((0, 352), (352, 416))
-SCALAR_WEAVES = ((416, 576), (576, 800), (800, 1024))
+SCALAR_WEAVES = ((416, 608), (608, 832), (832, 1024))
 PIECES = ((0, 128), (128, 256), (256, 384), (384, 512), (512, 640), (640, 768), (768, 896), (896, 1024))
 
 

@@ -136,18 +136,15 @@ def tile_routed_moe_kernel(tc, xT, w_words, w_scales, b, gate, offs, pos1, pos2,
                 nc.scalar.activation(y[:, cols], acc[:], GELU, bias=b_t[:, e : e + 1])
 
         first = keep.tile([P, T], F32, name="first")
+        fetched = keep.tile([P, T], F32, name="fetched")
         second = keep.tile([P, T], F32, name="second")
         total = keep.tile([P, T], F32, name="total")
-        half = T // 2
+        ranges = [slice(lo, lo + HALF) for lo in (0, HALF)]
+        for cols in ranges:
+            nc.scalar.activation(fetched[:, cols], y[:].indirect(pos2_t[:, cols.start // 16 : cols.stop // 16]), COPY)
         nc.vector.tensor_tensor(first[:], y[:].indirect(pos1_t[:]), gates[:, 0, :], MULT)
-        for lo in (0, half):
-            nc.vector.tensor_tensor(
-                second[:, lo : lo + half],
-                y[:].indirect(pos2_t[:, lo // 16 : (lo + half) // 16]),
-                gates[:, 1, lo : lo + half],
-                MULT,
-            )
-        for lo in (0, half):
-            cols = slice(lo, lo + half)
+        for cols in ranges:
+            nc.vector.tensor_tensor(second[:, cols], fetched[:, cols], gates[:, 1, cols], MULT)
+        for cols in ranges:
             nc.vector.tensor_add(total[:, cols], first[:, cols], second[:, cols])
             nc.sync.dma_start(out[:, cols], total[:, cols])

@@ -22,14 +22,14 @@ ADD = mybir.AluOpType.add
 R = 4
 HALF = T // 2
 LAST = 384
-VEC_CAST = 320
-VEC_SLOTS = 256
-DIRECT_HIGH = ((0, 352),)
-SCALAR_GATHERS = ((256, 640), (640, 1024))
-GATHERS = ((352, 608), (608, 832), (832, 1024))
-POOL_WEAVES = ((0, 352), (352, 416))
-SCALAR_WEAVES = ((416, 608), (608, 832), (832, 1024))
-PIECES = ((0, 128), (128, 256), (256, 384), (384, 512), (512, 640), (640, 768), (768, 896), (896, 1024))
+VEC_LOW = 192
+DIRECT_HIGH = 224
+WIDE = 1664
+ROW0_CUTS = ((192, 1024),)
+ROW1_CUTS = ((192, 512), (512, 1024))
+WORD_CUTS = ((224, 512), (512, 800), (800, 1024))
+POOL_WEAVES = ((0, 192), (192, 512))
+SCALAR_WEAVES = ((512, 800), (800, 1024))
 
 
 def tile_routed_moe_kernel(tc, xT, w_words, w_scales, b, gate, offs, pos1, pos2, out):
@@ -43,15 +43,17 @@ def tile_routed_moe_kernel(tc, xT, w_words, w_scales, b, gate, offs, pos1, pos2,
         nc.scalar.activation(warm[:], warm[:], GELU)
 
         x_rows = xT.rearrange("(p r) w -> p r w", r=R)
-        raw = keep.tile([P, R, T], F32, name="raw")
+        x_high = xT.rearrange("(p r) w -> p (r w)", r=R)[:, 2 * T :]
+        row0 = keep.tile([P, WIDE], F32, name="row0")
+        row1 = keep.tile([P, WIDE], F32, name="row1")
+        rows23 = keep.tile([P, 2, T], F32, name="rows23")
+        run23 = rows23[:].rearrange("p r w -> p (r w)")
         offs_t = keep.tile([P, SLOTS // 16], U16, name="offs_t")
-        nc.sync.dma_start(raw[:, 0, :], x_rows[:, 0, :])
+        nc.sync.dma_start(row0[:, :T], x_rows[:, 0, :])
         nc.sync.dma_start(offs_t[:], offs)
-        nc.sync.dma_start(raw[:, 1, :], x_rows[:, 1, :])
-        x_runs = xT.rearrange("(p r) w -> p (r w)", r=R)
-        rows = raw[:].rearrange("p r w -> p (r w)")
-        nc.sync.dma_start(rows[:, 2 * T + LAST :], x_runs[:, 2 * T + LAST :])
-        nc.sync.dma_start(rows[:, 2 * T : 2 * T + LAST], x_runs[:, 2 * T : 2 * T + LAST])
+        nc.sync.dma_start(run23[:, LAST:], x_high[:, LAST:])
+        nc.sync.dma_start(run23[:, :LAST], x_high[:, :LAST])
+        nc.sync.dma_start(row1[:, :T], x_rows[:, 1, :])
 
         w_s = keep.tile([P, E * N], U8, name="w_s", align_bytes=64)
         nc.vector.memset(w_s[:].bitcast(I32), 0)
@@ -74,10 +76,7 @@ def tile_routed_moe_kernel(tc, xT, w_words, w_scales, b, gate, offs, pos1, pos2,
         gates = keep.tile([P, 2, T], F32, name="gates")
         nc.sync.dma_start(gates[:], gate.rearrange("s p t -> p s t"))
 
-        plane0 = keep.tile([P, T], BF16, name="plane0")
-        plane1 = keep.tile([P, T], BF16, name="plane1")
-        high_t = keep.tile([P, T], I32, name="high_t")
-        high_pairs = high_t[:]
+        high_words = keep.tile([P, T], I32, name="high_words")
         picked = keep.tile([P, 2, SLOTS], U32, name="picked")
         grouped = keep.tile([P, SLOTS, 2], U32, name="grouped", align_bytes=64)
         slot_codes = keep.tile([P, SLOTS], U32, name="slot_codes", align_bytes=64)
@@ -90,50 +89,44 @@ def tile_routed_moe_kernel(tc, xT, w_words, w_scales, b, gate, offs, pos1, pos2,
         def entries(lo, hi):
             return offs_t[:, lo // 16 : hi // 16]
 
-        def cast_high(lo, hi):
-            return halves(high_pairs[:, lo:hi]), raw[:, 2:4, lo:hi].rearrange("p r w -> p w r")
-
         low = halves(picked[:, 0, :])
         high = halves(picked[:, 1, :])
-        nc.vector.tensor_copy(plane0[:, :VEC_CAST], raw[:, 0, :VEC_CAST])
-        nc.scalar.copy(plane0[:, VEC_CAST:], raw[:, 0, VEC_CAST:])
-        nc.gpsimd.tensor_scalar(plane1[:], raw[:, 1, :], 1.0, 0.0, MULT, ADD)
-        nc.gpsimd.tensor_scalar(*cast_high(LAST, T), 1.0, 0.0, MULT, ADD)
-        nc.gpsimd.tensor_scalar(*cast_high(0, LAST), 1.0, 0.0, MULT, ADD)
-        for r in (0, 1):
-            nc.vector.tensor_copy(low[:, :VEC_SLOTS, r], raw[:, r, :].indirect(entries(0, VEC_SLOTS)))
-        for r in (3, 2):
-            for lo, hi in DIRECT_HIGH:
-                nc.vector.tensor_copy(high[:, lo:hi, r - 2], raw[:, r, :].indirect(entries(lo, hi)))
-        for r, plane in enumerate((plane0, plane1)):
-            for lo, hi in SCALAR_GATHERS:
-                nc.scalar.activation(low[:, lo:hi, r], plane[:].indirect(entries(lo, hi)), COPY)
+        for lo, hi in ((LAST, T), (0, LAST)):
+            nc.gpsimd.tensor_scalar(
+                halves(high_words[:, lo:hi]), rows23[:, :, lo:hi].rearrange("p r w -> p w r"), 1.0, 0.0, MULT, ADD
+            )
+        nc.vector.tensor_copy(low[:, :VEC_LOW, 0], row0[:, :T].indirect(entries(0, VEC_LOW)))
+        for r in (1, 0):
+            nc.vector.tensor_copy(high[:, :DIRECT_HIGH, r], rows23[:, r, :].indirect(entries(0, DIRECT_HIGH)))
+        nc.vector.tensor_copy(low[:, :VEC_LOW, 1], row1[:, :T].indirect(entries(0, VEC_LOW)))
+        for r, (row, cuts) in enumerate(((row0, ROW0_CUTS), (row1, ROW1_CUTS))):
+            for lo, hi in cuts:
+                nc.scalar.activation(low[:, lo:hi, r], row[:].indirect(entries(lo, hi)), COPY)
 
-        for lo, hi in GATHERS:
-            nc.vector.tensor_copy(picked[:, 1, lo:hi], high_pairs.bitcast(U32).indirect(entries(lo, hi)))
+        for lo, hi in WORD_CUTS:
+            nc.vector.tensor_copy(picked[:, 1, lo:hi], high_words[:].bitcast(U32).indirect(entries(lo, hi)))
         for lo, hi in POOL_WEAVES:
             nc.gpsimd.tensor_copy(grouped[:, lo:hi, :], picked[:, :, lo:hi].rearrange("p u s -> p s u"))
         for lo, hi in SCALAR_WEAVES:
             nc.scalar.copy(grouped[:, lo:hi, :], picked[:, :, lo:hi].rearrange("p u s -> p s u"))
-        for lo, hi in PIECES:
+        for e in range(E):
+            cols = slice(e * C, (e + 1) * C)
             nc.vector.quantize_mx(
-                out=slot_codes[:, lo:hi].bitcast(FP8X4),
-                scales=slot_scales[:, lo:hi],
-                in_=grouped[:, lo:hi, :].rearrange("p s u -> p (s u)").bitcast(BF16),
+                out=slot_codes[:, cols].bitcast(FP8X4),
+                scales=slot_scales[:, cols],
+                in_=grouped[:, cols, :].rearrange("p s u -> p (s u)").bitcast(BF16),
             )
-            for e in range(lo // C, hi // C):
-                cols = slice(e * C, (e + 1) * C)
-                acc = psum.tile([N, C], F32, name=f"acc{e}")
-                nc.tensor.matmul_mx(
-                    out=acc[:],
-                    lhsT=w_c[:, cols].bitcast(FP8X4),
-                    lhsT_scale=w_s[:, cols],
-                    rhs=slot_codes[:, cols].bitcast(FP8X4),
-                    rhs_scale=slot_scales[:, cols],
-                    start=True,
-                    stop=True,
-                )
-                nc.scalar.activation(y[:, cols], acc[:], GELU, bias=b_t[:, e : e + 1])
+            acc = psum.tile([N, C], F32, name=f"acc{e}")
+            nc.tensor.matmul_mx(
+                out=acc[:],
+                lhsT=w_c[:, cols].bitcast(FP8X4),
+                lhsT_scale=w_s[:, cols],
+                rhs=slot_codes[:, cols].bitcast(FP8X4),
+                rhs_scale=slot_scales[:, cols],
+                start=True,
+                stop=True,
+            )
+            nc.scalar.activation(y[:, cols], acc[:], GELU, bias=b_t[:, e : e + 1])
 
         first = keep.tile([P, T], F32, name="first")
         fetched = keep.tile([P, T], F32, name="fetched")

@@ -22,14 +22,15 @@ ADD = mybir.AluOpType.add
 R = 4
 HALF = T // 2
 LAST = 384
-VEC_LOW = 192
-DIRECT_HIGH = 224
-WIDE = 1664
-ROW0_CUTS = ((192, 1024),)
-ROW1_CUTS = ((192, 512), (512, 1024))
-WORD_CUTS = ((224, 512), (512, 800), (800, 1024))
-POOL_WEAVES = ((0, 192), (192, 512))
-SCALAR_WEAVES = ((512, 800), (800, 1024))
+VEC_LOW = (288, 480)
+DIRECT_HIGH = (288, 512)
+EXPERT_ORDER = (3, 4, 5, 0, 1, 2, 6, 7)
+WIDE = 1088
+ROW0_CUTS = ((480, 1024), (0, 288))
+ROW1_CUTS = ((480, 800), (800, 1024), (0, 288))
+WORD_CUTS = ((512, 800), (0, 288), (800, 1024))
+POOL_WEAVES = ((288, 480), (480, 800))
+SCALAR_WEAVES = ((0, 288), (800, 1024))
 
 
 def tile_routed_moe_kernel(tc, xT, w_words, w_scales, b, gate, offs, pos1, pos2, out):
@@ -95,10 +96,10 @@ def tile_routed_moe_kernel(tc, xT, w_words, w_scales, b, gate, offs, pos1, pos2,
             nc.gpsimd.tensor_scalar(
                 halves(high_words[:, lo:hi]), rows23[:, :, lo:hi].rearrange("p r w -> p w r"), 1.0, 0.0, MULT, ADD
             )
-        nc.vector.tensor_copy(low[:, :VEC_LOW, 0], row0[:, :T].indirect(entries(0, VEC_LOW)))
+        nc.vector.tensor_copy(low[:, slice(*VEC_LOW), 0], row0[:, :T].indirect(entries(*VEC_LOW)))
         for r in (1, 0):
-            nc.vector.tensor_copy(high[:, :DIRECT_HIGH, r], rows23[:, r, :].indirect(entries(0, DIRECT_HIGH)))
-        nc.vector.tensor_copy(low[:, :VEC_LOW, 1], row1[:, :T].indirect(entries(0, VEC_LOW)))
+            nc.vector.tensor_copy(high[:, slice(*DIRECT_HIGH), r], rows23[:, r, :].indirect(entries(*DIRECT_HIGH)))
+        nc.vector.tensor_copy(low[:, slice(*VEC_LOW), 1], row1[:, :T].indirect(entries(*VEC_LOW)))
         for r, (row, cuts) in enumerate(((row0, ROW0_CUTS), (row1, ROW1_CUTS))):
             for lo, hi in cuts:
                 nc.scalar.activation(low[:, lo:hi, r], row[:].indirect(entries(lo, hi)), COPY)
@@ -109,7 +110,7 @@ def tile_routed_moe_kernel(tc, xT, w_words, w_scales, b, gate, offs, pos1, pos2,
             nc.gpsimd.tensor_copy(grouped[:, lo:hi, :], picked[:, :, lo:hi].rearrange("p u s -> p s u"))
         for lo, hi in SCALAR_WEAVES:
             nc.scalar.copy(grouped[:, lo:hi, :], picked[:, :, lo:hi].rearrange("p u s -> p s u"))
-        for e in range(E):
+        for e in EXPERT_ORDER:
             cols = slice(e * C, (e + 1) * C)
             nc.vector.quantize_mx(
                 out=slot_codes[:, cols].bitcast(FP8X4),

@@ -22,15 +22,16 @@ ADD = mybir.AluOpType.add
 R = 4
 HALF = T // 2
 LAST = 384
-VEC_LOW = (288, 480)
-DIRECT_HIGH = (288, 512)
-EXPERT_ORDER = (3, 4, 5, 0, 1, 2, 6, 7)
-WIDE = 1088
-ROW0_CUTS = ((480, 1024), (0, 288))
-ROW1_CUTS = ((480, 800), (800, 1024), (0, 288))
-WORD_CUTS = ((512, 800), (0, 288), (800, 1024))
-POOL_WEAVES = ((288, 480), (480, 800))
-SCALAR_WEAVES = ((0, 288), (800, 1024))
+VEC_LOW = (0, 256)
+DIRECT_HIGH = (0, 256)
+FETCH_CUTS = ((0, 352), (352, 512))
+EXPERT_ORDER = (0, 1, 2, 3, 4, 5, 6, 7)
+WIDE = 1536
+ROW0_CUTS = ((256, 1024),)
+ROW1_CUTS = ((256, 512), (512, 1024))
+WORD_CUTS = ((256, 512), (512, 768), (768, 1024))
+POOL_WEAVES = ((8, 248), (248, 512))
+SCALAR_WEAVES = ((0, 8), (512, 768), (768, 1024))
 
 
 def tile_routed_moe_kernel(tc, xT, w_words, w_scales, b, gate, offs, pos1, pos2, out):
@@ -134,11 +135,11 @@ def tile_routed_moe_kernel(tc, xT, w_words, w_scales, b, gate, offs, pos1, pos2,
         second = keep.tile([P, T], F32, name="second")
         total = keep.tile([P, T], F32, name="total")
         ranges = [slice(lo, lo + HALF) for lo in (0, HALF)]
-        for cols in ranges:
-            nc.scalar.activation(fetched[:, cols], y[:].indirect(pos2_t[:, cols.start // 16 : cols.stop // 16]), COPY)
+        for lo, hi in FETCH_CUTS:
+            nc.scalar.activation(fetched[:, lo:hi], y[:].indirect(pos2_t[:, lo // 16 : hi // 16]), COPY)
         nc.vector.tensor_tensor(first[:], y[:].indirect(pos1_t[:]), gates[:, 0, :], MULT)
-        for cols in ranges:
-            nc.vector.tensor_tensor(second[:, cols], fetched[:, cols], gates[:, 1, cols], MULT)
+        for lo, hi in FETCH_CUTS:
+            nc.vector.tensor_tensor(second[:, lo:hi], fetched[:, lo:hi], gates[:, 1, lo:hi], MULT)
         for cols in ranges:
             nc.vector.tensor_add(total[:, cols], first[:, cols], second[:, cols])
             nc.sync.dma_start(out[:, cols], total[:, cols])

@@ -23,14 +23,14 @@ R = 4
 HALF = T // 2
 LAST = 384
 VEC_LOW = (0, 256)
-DIRECT_HIGH = (0, 256)
+DIRECT_HIGH = (0, 224)
 FETCH_CUTS = ((0, 352), (352, 512))
 EXPERT_ORDER = (0, 1, 2, 3, 4, 5, 6, 7)
 WIDE = 1536
 ROW0_CUTS = ((256, 1024),)
 ROW1_CUTS = ((256, 512), (512, 1024))
-WORD_CUTS = ((256, 512), (512, 768), (768, 1024))
-POOL_WEAVES = ((8, 248), (248, 512))
+WORD_CUTS = ((224, 512), (512, 768), (768, 1024))
+POOL_WEAVES = ((8, 224), (224, 512))
 SCALAR_WEAVES = ((0, 8), (512, 768), (768, 1024))
 
 

@@ -43,6 +43,12 @@ def tile_routed_moe_kernel(tc, xT, w_words, w_scales, b, gate, offs, pos1, pos2,
         warm = keep.tile([P, 1], F32, name="warm")
         nc.vector.memset(warm[:], 0.0)
         nc.scalar.activation(warm[:], warm[:], GELU)
+        zeros = keep.tile([P, 2, 8], F32, name="zeros")
+        nc.vector.memset(zeros[:], 0.0)
+        warm_cast = keep.tile([P, 8, 2], BF16, name="warm_cast")
+        nc.gpsimd.tensor_scalar(warm_cast[:], zeros[:].rearrange("p r w -> p w r"), 1.0, 0.0, MULT, ADD)
+        warm_copy = keep.tile([P, 8, 2], U32, name="warm_copy")
+        nc.gpsimd.tensor_copy(warm_copy[:], zeros[:].bitcast(U32).rearrange("p u s -> p s u"))
 
         x_rows = xT.rearrange("(p r) w -> p r w", r=R)
         x_high = xT.rearrange("(p r) w -> p (r w)", r=R)[:, 2 * T :]

@@ -52,9 +52,9 @@ def tile_routed_moe_kernel(tc, xT, w_words, w_scales, b, gate, offs, pos1, pos2,
 
         x_rows = xT.rearrange("(p r) w -> p r w", r=R)
         x_high = xT.rearrange("(p r) w -> p (r w)", r=R)[:, 2 * T :]
-        row0 = keep.tile([P, WIDE], F32, name="row0")
-        row1 = keep.tile([P, WIDE], F32, name="row1")
-        rows23 = keep.tile([P, 2, T], F32, name="rows23")
+        row0 = keep.tile([P, WIDE], F32, name="row0", align_bytes=256)
+        row1 = keep.tile([P, WIDE], F32, name="row1", align_bytes=256)
+        rows23 = keep.tile([P, 2, T], F32, name="rows23", align_bytes=256)
         run23 = rows23[:].rearrange("p r w -> p (r w)")
         offs_t = keep.tile([P, SLOTS // 16], U16, name="offs_t")
         nc.sync.dma_start(row0[:, :T], x_rows[:, 0, :])
@@ -63,14 +63,14 @@ def tile_routed_moe_kernel(tc, xT, w_words, w_scales, b, gate, offs, pos1, pos2,
         nc.sync.dma_start(run23[:, :LAST], x_high[:, :LAST])
         nc.sync.dma_start(row1[:, :T], x_rows[:, 1, :])
 
-        w_s = keep.tile([P, E * N], U8, name="w_s", align_bytes=64)
+        w_s = keep.tile([P, E * N], U8, name="w_s", align_bytes=256)
         nc.vector.memset(w_s[:].bitcast(I32), 0)
         for q in range(4):
             nc.sync.dma_start(
                 w_s[32 * q : 32 * q + 4, :].bitcast(I32).rearrange("p (e n) -> p e n", e=E),
                 w_scales[:, 0, 4 * q : 4 * q + 4, :].rearrange("e q n -> q e n").bitcast(I32),
             )
-        w_c = keep.tile([P, E * N], U32, name="w_c", align_bytes=64)
+        w_c = keep.tile([P, E * N], U32, name="w_c", align_bytes=256)
         nc.sync.dma_start(
             w_c[:].bitcast(I32).rearrange("p (e n) -> p e n", e=E),
             w_words.rearrange("e a p n r -> p (e a) (n r)").bitcast(I32),
@@ -81,15 +81,15 @@ def tile_routed_moe_kernel(tc, xT, w_words, w_scales, b, gate, offs, pos1, pos2,
         nc.sync.dma_start(pos1_t[:], pos1)
         pos2_t = keep.tile([P, T // 16], U16, name="pos2_t")
         nc.sync.dma_start(pos2_t[:], pos2)
-        gates = keep.tile([P, 2, T], F32, name="gates")
+        gates = keep.tile([P, 2, T], F32, name="gates", align_bytes=256)
         nc.sync.dma_start(gates[:], gate.rearrange("s p t -> p s t"))
 
-        high_words = keep.tile([P, T], I32, name="high_words")
-        picked = keep.tile([P, 2, SLOTS], U32, name="picked")
-        grouped = keep.tile([P, SLOTS, 2], U32, name="grouped", align_bytes=64)
-        slot_codes = keep.tile([P, SLOTS], U32, name="slot_codes", align_bytes=64)
-        slot_scales = keep.tile([P, SLOTS], U8, name="slot_scales", align_bytes=64)
-        y = keep.tile([P, SLOTS], F32, name="y")
+        high_words = keep.tile([P, T], I32, name="high_words", align_bytes=256)
+        picked = keep.tile([P, 2, SLOTS], U32, name="picked", align_bytes=256)
+        grouped = keep.tile([P, SLOTS, 2], U32, name="grouped", align_bytes=256)
+        slot_codes = keep.tile([P, SLOTS], U32, name="slot_codes", align_bytes=256)
+        slot_scales = keep.tile([P, SLOTS], U8, name="slot_scales", align_bytes=256)
+        y = keep.tile([P, SLOTS], F32, name="y", align_bytes=256)
 
         def halves(words):
             return words.bitcast(BF16).rearrange("p (w r) -> p w r", r=2)
@@ -136,10 +136,10 @@ def tile_routed_moe_kernel(tc, xT, w_words, w_scales, b, gate, offs, pos1, pos2,
             )
             nc.scalar.activation(y[:, cols], acc[:], GELU, bias=b_t[:, e : e + 1])
 
-        first = keep.tile([P, T], F32, name="first")
-        fetched = keep.tile([P, T], F32, name="fetched")
-        second = keep.tile([P, T], F32, name="second")
-        total = keep.tile([P, T], F32, name="total")
+        first = keep.tile([P, T], F32, name="first", align_bytes=256)
+        fetched = keep.tile([P, T], F32, name="fetched", align_bytes=256)
+        second = keep.tile([P, T], F32, name="second", align_bytes=256)
+        total = keep.tile([P, T], F32, name="total", align_bytes=256)
         ranges = [slice(lo, lo + HALF) for lo in (0, HALF)]
         for lo, hi in FETCH_CUTS:
             nc.scalar.activation(fetched[:, lo:hi], y[:].indirect(pos2_t[:, lo // 16 : hi // 16]), COPY)

@@ -22,13 +22,13 @@ ADD = mybir.AluOpType.add
 R = 4
 HALF = T // 2
 LAST = 384
-VEC_LOW = (0, 256)
+VEC_LOW = (0, 224)
 DIRECT_HIGH = (0, 224)
 FETCH_CUTS = ((0, 352), (352, 512))
 EXPERT_ORDER = (0, 1, 2, 3, 4, 5, 6, 7)
-WIDE = 1536
-ROW0_CUTS = ((256, 1024),)
-ROW1_CUTS = ((256, 512), (512, 1024))
+WIDE = 1600
+ROW0_CUTS = ((224, 1024),)
+ROW1_CUTS = ((224, 512), (512, 1024))
 WORD_CUTS = ((224, 512), (512, 768), (768, 1024))
 POOL_WEAVES = ((8, 224), (224, 512))
 SCALAR_WEAVES = ((0, 8), (512, 768), (768, 1024))

@@ -28,10 +28,10 @@ FETCH_CUTS = ((0, 352), (352, 512))
 EXPERT_ORDER = (0, 1, 2, 3, 4, 5, 6, 7)
 WIDE = 1600
 ROW0_CUTS = ((224, 1024),)
-ROW1_CUTS = ((224, 512), (512, 1024))
-WORD_CUTS = ((224, 512), (512, 768), (768, 1024))
-POOL_WEAVES = ((8, 224), (224, 512))
-SCALAR_WEAVES = ((0, 8), (512, 768), (768, 1024))
+ROW1_CUTS = ((224, 544), (544, 1024))
+WORD_CUTS = ((224, 544), (544, 800), (800, 1024))
+POOL_WEAVES = ((8, 224), (224, 544))
+SCALAR_WEAVES = ((0, 8), (544, 800), (800, 1024))
 
 
 def tile_routed_moe_kernel(tc, xT, w_words, w_scales, b, gate, offs, pos1, pos2, out):

from contextlib import ExitStack

import concourse.mybir as mybir

K, T, E, C, N = 512, 512, 8, 128, 128
P = 128
SLOTS = E * C
FLOPS = 2 * K * SLOTS * N

F32 = mybir.dt.float32
BF16 = mybir.dt.bfloat16
I32 = mybir.dt.int32
U32 = mybir.dt.uint32
U16 = mybir.dt.uint16
U8 = mybir.dt.uint8
FP8X4 = mybir.dt.float8_e4m3fn_x4
GELU = mybir.ActivationFunctionType.Gelu_apprx_tanh
COPY = mybir.ActivationFunctionType.Copy
MULT = mybir.AluOpType.mult
ADD = mybir.AluOpType.add

R = 4
HALF = T // 2
LAST = 384
VEC_LOW = (0, 224)
DIRECT_HIGH = (0, 224)
FETCH_CUTS = ((0, 352), (352, 512))
EXPERT_ORDER = (0, 1, 2, 3, 4, 5, 6, 7)
WIDE = 1600
ROW0_CUTS = ((224, 1024),)
ROW1_CUTS = ((224, 544), (544, 1024))
WORD_CUTS = ((224, 544), (544, 800), (800, 1024))
POOL_WEAVES = ((8, 224), (224, 544))
SCALAR_WEAVES = ((0, 8), (544, 800), (800, 1024))


def tile_routed_moe_kernel(tc, xT, w_words, w_scales, b, gate, offs, pos1, pos2, out):
    nc = tc.nc
    with ExitStack() as ctx:
        keep = ctx.enter_context(tc.tile_pool(name="keep", bufs=1))
        psum = ctx.enter_context(tc.psum_pool(name="psum", bufs=1))

        warm = keep.tile([P, 1], F32, name="warm")
        nc.vector.memset(warm[:], 0.0)
        nc.scalar.activation(warm[:], warm[:], GELU)
        zeros = keep.tile([P, 2, 8], F32, name="zeros")
        nc.vector.memset(zeros[:], 0.0)
        warm_cast = keep.tile([P, 8, 2], BF16, name="warm_cast")
        nc.gpsimd.tensor_scalar(warm_cast[:], zeros[:].rearrange("p r w -> p w r"), 1.0, 0.0, MULT, ADD)
        warm_copy = keep.tile([P, 8, 2], U32, name="warm_copy")
        nc.gpsimd.tensor_copy(warm_copy[:], zeros[:].bitcast(U32).rearrange("p u s -> p s u"))

        x_rows = xT.rearrange("(p r) w -> p r w", r=R)
        x_high = xT.rearrange("(p r) w -> p (r w)", r=R)[:, 2 * T :]
        row0 = keep.tile([P, WIDE], F32, name="row0", align_bytes=256)
        row1 = keep.tile([P, WIDE], F32, name="row1", align_bytes=256)
        rows23 = keep.tile([P, 2, T], F32, name="rows23", align_bytes=256)
        run23 = rows23[:].rearrange("p r w -> p (r w)")
        offs_t = keep.tile([P, SLOTS // 16], U16, name="offs_t")
        nc.sync.dma_start(row0[:, :T], x_rows[:, 0, :])
        nc.sync.dma_start(offs_t[:], offs)
        nc.sync.dma_start(run23[:, LAST:], x_high[:, LAST:])
        nc.sync.dma_start(run23[:, :LAST], x_high[:, :LAST])
        nc.sync.dma_start(row1[:, :T], x_rows[:, 1, :])

        w_s = keep.tile([P, E * N], U8, name="w_s", align_bytes=256)
        nc.vector.memset(w_s[:].bitcast(I32), 0)
        for q in range(4):
            nc.sync.dma_start(
                w_s[32 * q : 32 * q + 4, :].bitcast(I32).rearrange("p (e n) -> p e n", e=E),
                w_scales[:, 0, 4 * q : 4 * q + 4, :].rearrange("e q n -> q e n").bitcast(I32),
            )
        w_c = keep.tile([P, E * N], U32, name="w_c", align_bytes=256)
        nc.sync.dma_start(
            w_c[:].bitcast(I32).rearrange("p (e n) -> p e n", e=E),
            w_words.rearrange("e a p n r -> p (e a) (n r)").bitcast(I32),
        )
        b_t = keep.tile([P, E], F32, name="b_t")
        nc.sync.dma_start(b_t[:], b)
        pos1_t = keep.tile([P, T // 16], U16, name="pos1_t")
        nc.sync.dma_start(pos1_t[:], pos1)
        pos2_t = keep.tile([P, T // 16], U16, name="pos2_t")
        nc.sync.dma_start(pos2_t[:], pos2)
        gates = keep.tile([P, 2, T], F32, name="gates", align_bytes=256)
        nc.sync.dma_start(gates[:], gate.rearrange("s p t -> p s t"))

        high_words = keep.tile([P, T], I32, name="high_words", align_bytes=256)
        picked = keep.tile([P, 2, SLOTS], U32, name="picked", align_bytes=256)
        grouped = keep.tile([P, SLOTS, 2], U32, name="grouped", align_bytes=256)
        slot_codes = keep.tile([P, SLOTS], U32, name="slot_codes", align_bytes=256)
        slot_scales = keep.tile([P, SLOTS], U8, name="slot_scales", align_bytes=256)
        y = keep.tile([P, SLOTS], F32, name="y", align_bytes=256)

        def halves(words):
            return words.bitcast(BF16).rearrange("p (w r) -> p w r", r=2)

        def entries(lo, hi):
            return offs_t[:, lo // 16 : hi // 16]

        low = halves(picked[:, 0, :])
        high = halves(picked[:, 1, :])
        for lo, hi in ((LAST, T), (0, LAST)):
            nc.gpsimd.tensor_scalar(
                halves(high_words[:, lo:hi]), rows23[:, :, lo:hi].rearrange("p r w -> p w r"), 1.0, 0.0, MULT, ADD
            )
        nc.vector.tensor_copy(low[:, slice(*VEC_LOW), 0], row0[:, :T].indirect(entries(*VEC_LOW)))
        for r in (1, 0):
            nc.vector.tensor_copy(high[:, slice(*DIRECT_HIGH), r], rows23[:, r, :].indirect(entries(*DIRECT_HIGH)))
        nc.vector.tensor_copy(low[:, slice(*VEC_LOW), 1], row1[:, :T].indirect(entries(*VEC_LOW)))
        for r, (row, cuts) in enumerate(((row0, ROW0_CUTS), (row1, ROW1_CUTS))):
            for lo, hi in cuts:
                nc.scalar.activation(low[:, lo:hi, r], row[:].indirect(entries(lo, hi)), COPY)

        for lo, hi in WORD_CUTS:
            nc.vector.tensor_copy(picked[:, 1, lo:hi], high_words[:].bitcast(U32).indirect(entries(lo, hi)))
        for lo, hi in POOL_WEAVES:
            nc.gpsimd.tensor_copy(grouped[:, lo:hi, :], picked[:, :, lo:hi].rearrange("p u s -> p s u"))
        for lo, hi in SCALAR_WEAVES:
            nc.scalar.copy(grouped[:, lo:hi, :], picked[:, :, lo:hi].rearrange("p u s -> p s u"))
        for e in EXPERT_ORDER:
            cols = slice(e * C, (e + 1) * C)
            nc.vector.quantize_mx(
                out=slot_codes[:, cols].bitcast(FP8X4),
                scales=slot_scales[:, cols],
                in_=grouped[:, cols, :].rearrange("p s u -> p (s u)").bitcast(BF16),
            )
            acc = psum.tile([N, C], F32, name=f"acc{e}")
            nc.tensor.matmul_mx(
                out=acc[:],
                lhsT=w_c[:, cols].bitcast(FP8X4),
                lhsT_scale=w_s[:, cols],
                rhs=slot_codes[:, cols].bitcast(FP8X4),
                rhs_scale=slot_scales[:, cols],
                start=True,
                stop=True,
            )
            nc.scalar.activation(y[:, cols], acc[:], GELU, bias=b_t[:, e : e + 1])

        first = keep.tile([P, T], F32, name="first", align_bytes=256)
        fetched = keep.tile([P, T], F32, name="fetched", align_bytes=256)
        second = keep.tile([P, T], F32, name="second", align_bytes=256)
        total = keep.tile([P, T], F32, name="total", align_bytes=256)
        ranges = [slice(lo, lo + HALF) for lo in (0, HALF)]
        for lo, hi in FETCH_CUTS:
            nc.scalar.activation(fetched[:, lo:hi], y[:].indirect(pos2_t[:, lo // 16 : hi // 16]), COPY)
        nc.vector.tensor_tensor(first[:], y[:].indirect(pos1_t[:]), gates[:, 0, :], MULT)
        for lo, hi in FETCH_CUTS:
            nc.vector.tensor_tensor(second[:, lo:hi], fetched[:, lo:hi], gates[:, 1, lo:hi], MULT)
        for cols in ranges:
            nc.vector.tensor_add(total[:, cols], first[:, cols], second[:, cols])
            nc.sync.dma_start(out[:, cols], total[:, cols])
